import numpy as np
import ml_dtypes


def mxq(x, axis, fmt="e4m3"):
    dtype, down = {"e4m3": (ml_dtypes.float8_e4m3fn, 7), "e5m2": (ml_dtypes.float8_e5m2, 14)}[fmt]
    v = np.moveaxis(np.asarray(x, np.float32).astype(ml_dtypes.bfloat16).astype(np.float64), axis, -1)
    blocks = v.reshape(v.shape[:-1] + (-1, 32))
    amax = np.abs(blocks).max(-1, keepdims=True)
    byte = np.maximum(np.where(amax > 0, np.frexp(amax)[1] - 1 + 127, 0) - down, 1)
    scale = np.exp2(byte - 127.0)
    codes = (blocks / scale).astype(np.float32).astype(dtype).astype(np.float64)
    return np.moveaxis((codes * scale).reshape(v.shape), -1, axis)


WIDE = False


def mx_kscale(k):
    if not WIDE:
        return np.ones(k)
    levels = np.array([24, -24, 12, -12, 0])
    if k % 512:
        return np.exp2(np.random.permutation(np.resize(levels, k // 32))).repeat(32)
    a = np.empty((k // 512, 16))
    for p in range(k // 512):
        a[p, :8] = np.random.permutation(np.resize(levels, 8))
        for g in range(8):
            far = levels[np.abs(levels - a[p, g]) >= 10]
            a[p, g + 8] = far[np.random.randint(len(far))]
    return np.exp2(a.ravel()).repeat(32)


def f64(x):
    return np.asarray(x).astype(np.float64)


def striped8(idx):
    return np.concatenate([v.reshape(-1, 16).T for v in idx]).astype(np.uint16)


def unstriped8(offs):
    return np.stack([offs[16 * g:16 * g + 16].T.reshape(-1) for g in range(8)]).astype(np.int64)


E2M1 = np.array([0.0, 0.5, 1.0, 1.5, 2.0, 3.0, 4.0, 6.0, -0.0, -0.5, -1.0, -1.5, -2.0, -3.0, -4.0, -6.0])


def pack_weight(w, fmt):
    k, n = w.shape
    w = f64(np.asarray(w, np.float32).astype(ml_dtypes.bfloat16)).reshape(k // 32, 32, n)
    amax = np.abs(w).max(1)
    if fmt == "e4m3":
        byte = np.frexp(amax)[1] - 1 + 127 - 7
    else:
        mant, ex = np.frexp(amax / 6.0)
        byte = np.where(mant > 0.5, ex, ex - 1) + 127
    byte = np.clip(np.where(amax > 0, byte, 1), 1, 254)
    scaled = (w * np.exp2(127.0 - byte)[:, None, :]).reshape(k, n).astype(np.float32)
    by_word = np.ascontiguousarray(scaled.reshape(k // 512, 128, 4, n).transpose(0, 1, 3, 2))
    if fmt == "e4m3":
        words = by_word.astype(ml_dtypes.float8_e4m3fn).view(np.uint8)
    else:
        c = by_word.astype(ml_dtypes.float4_e2m1fn).view(np.uint8) & 0xF
        words = (c[..., 0::2] | (c[..., 1::2] << 4)).reshape(k // 512, 128, 2 * n)
    return np.ascontiguousarray(words), np.ascontiguousarray(byte.astype(np.uint8).reshape(k // 512, 16, n))


def unpack_weight(words, scales, fmt):
    g, _, n = scales.shape
    words = np.ascontiguousarray(words).reshape(g, 128, n, -1)
    if fmt == "e4m3":
        vals = words.view(ml_dtypes.float8_e4m3fn).astype(np.float64)
    else:
        nib = np.empty((g, 128, n, 4), np.uint8)
        nib[..., 0::2] = words & 0xF
        nib[..., 1::2] = words >> 4
        vals = E2M1[nib]
    vals = vals * np.repeat(np.exp2(scales.astype(np.float64) - 127.0), 8, axis=1)[..., None]
    return vals.transpose(0, 1, 3, 2).reshape(g * 512, n)


def planes(y):
    n, m = y.shape
    v = y.astype(np.float32).astype(ml_dtypes.bfloat16).astype(np.float64).reshape(n // 32, 32, m)
    top = np.abs(v).max(1)
    byte = np.clip(np.where(top > 0, np.frexp(top)[1] - 1 + 127 - 7, 1), 1, 254)
    codes = (v * np.exp2(127.0 - byte)[:, None, :]).reshape(n, m).astype(np.float32).astype(ml_dtypes.float8_e4m3fn).view(np.uint8)
    words = codes.reshape(n // 512, 128, 4, m).transpose(0, 1, 3, 2)
    return np.ascontiguousarray(words), np.ascontiguousarray(byte.astype(np.uint8).reshape(n // 512, 16, m))


def sigm(f):
    return 1.0 / (1.0 + np.exp(-np.maximum(f, -700.0)))


K, N, T, J = 512, 512, 2048, 1024


def setup_inputs():
    n = np.random.standard_normal
    s = mx_kscale(K)[:, None]
    p_wv4 = pack_weight(n((K, N)) / np.sqrt(K) / s, "e2m1")
    return {
        "xT": (n((K, T)) * s).astype(np.float32),
        "wgt": np.repeat(np.random.uniform(0.5, 2.0, (8, J)), 16, axis=0).astype(np.float32),
        "wk": (n((K, N)) / np.sqrt(K) / s).astype(np.float32),
        "wv4_words": p_wv4[0],
        "wv4_scales": p_wv4[1],
        "wvd": (0.4 * (n((K, N)) / np.sqrt(K) / s)).astype(np.float32),
        "bg": (0.3 * n(N) - 1.0).astype(np.float32),
        "res": (n((N, J))).astype(np.float32),
        "offs": striped8(np.stack([np.random.permutation(T)[:J] for _ in range(8)])),
    }


def reference(xT, wgt, wk, wv4_words, wv4_scales, wvd, bg, res, offs):
    idx = unstriped8(offs)
    rows = np.arange(K)
    xg = f64(wgt)[rows // 4 % 128] * f64(xT)[rows[:, None], idx[rows % 512 // 64]]
    xT_ = mxq(xg, 0, "e4m3")
    wk_ = mxq(f64(wk), 0, "e4m3")
    wv4_ = unpack_weight(wv4_words, wv4_scales, "e2m1")
    wvd_ = mxq(f64(wvd), 0, "e4m3")
    ke = wk_.T @ xT_
    ve = wv4_.T @ xT_ + wvd_.T @ xT_
    gate = sigm(ke + f64(bg)[:, None])
    out_0 = f64(res) + gate * (np.tanh(ve) - f64(res))
    return (out_0,) + planes(out_0)

@@ -1,0 +1,241 @@
+from contextlib import ExitStack
+
+import concourse.mybir as mybir
+
+K, N, T, J = 512, 512, 2048, 1024
+FLOPS = 3 * 2 * K * N * J
+
+F32 = mybir.dt.float32
+BF16 = mybir.dt.bfloat16
+I32 = mybir.dt.int32
+U32 = mybir.dt.uint32
+U16 = mybir.dt.uint16
+U8 = mybir.dt.uint8
+FP8X4 = mybir.dt.float8_e4m3fn_x4
+FP4X4 = mybir.dt.float4_e2m1fn_x4
+ALU = mybir.AluOpType
+ACT = mybir.ActivationFunctionType
+
+P = 128
+PACK = 4
+HALF = 512
+HALVES = J // HALF
+WCOLS = 256
+PIECE = 256
+OUT_PIECES = ((256, 256), (256, 128, 128))
+
+
+def tile_list_dl_hwaytanhP_kernel(
+    tc, xT, wgt, wk, wv4_words, wv4_scales, wvd, bg, res, offs, out_0, out_1, out_2
+):
+    nc = tc.nc
+    with ExitStack() as ctx:
+        sb = ctx.enter_context(tc.tile_pool(name="sb", bufs=1))
+        psum = ctx.enter_context(tc.psum_pool(name="psum", bufs=4))
+
+        def tile(name, shape, dtype):
+            return sb.tile(shape, dtype, name=name, align_bytes=64)
+
+        offsets = sb.tile([P, J // 16], U16, name="offsets")
+        nc.sync.dma_start(offsets[:], offs)
+
+        x_rows = xT.rearrange("(p i) t -> p i t", i=PACK)
+        planes = [tile("plane%d" % i, [P, T], F32) for i in range(PACK)]
+        wgt_sb = [tile("wgt%d" % h, [P, HALF], F32) for h in range(HALVES)]
+        nc.sync.dma_start(wgt_sb[0][:], wgt[:, 0:HALF])
+        nc.sync.dma_start(planes[0][:], x_rows[:, 0, :])
+
+        s4_raw = tile("s4_raw", [P, N], U8)
+        nc.gpsimd.memset(s4_raw[:].bitcast(I32), 0)
+        w4_raw = tile("w4_raw", [P, 2 * N], U8)
+        nc.scalar.dma_start(w4_raw[:].bitcast(I32), wv4_words[0].bitcast(I32))
+        for q in range(4):
+            nc.scalar.dma_start(
+                s4_raw[32 * q : 32 * q + 4, :].bitcast(I32), wv4_scales[0, 4 * q : 4 * q + 4, :].bitcast(I32)
+            )
+
+        nc.sync.dma_start(wgt_sb[1][:], wgt[:, HALF:J])
+        for i in range(1, PACK):
+            nc.sync.dma_start(planes[i][:], x_rows[:, i, :])
+        bias = tile("bias", [P, PACK], F32)
+        nc.sync.dma_start(bias[:], bg.rearrange("(p t) -> p t", t=PACK))
+
+        warm = tile("warm", [P, 8], F32)
+        nc.vector.memset(warm[:], 0.0)
+        nc.scalar.activation(warm[:, 0:1], warm[:, 4:5], ACT.Sigmoid)
+
+        def load_weight(name, w, a):
+            raw = tile("%s_raw%d" % (name, a), [P, PACK, WCOLS], F32)
+            rows = w.rearrange("(p i) c -> p i c", i=PACK)
+            nc.sync.dma_start(raw[:], rows[:, :, a * WCOLS : (a + 1) * WCOLS])
+            return raw
+
+        res_rows = res.rearrange("(p t) j -> p t j", t=PACK)
+        res_sb = [tile("res%d" % h, [P, PACK, HALF], F32) for h in range(HALVES)]
+
+        def load_res(h, t):
+            nc.sync.dma_start(res_sb[h][:, t, :], res_rows[:, t, h * HALF : (h + 1) * HALF])
+
+        wk_raw = [load_weight("wk", wk, a) for a in range(2)]
+        load_res(0, 0)
+        wvd_raw = [load_weight("wvd", wvd, a) for a in range(2)]
+        for t in range(1, PACK):
+            load_res(0, t)
+        for t in range(PACK):
+            load_res(1, t)
+
+        w4_codes = tile("w4_codes", [P, 2 * N], U8)
+        nc.vector.tensor_copy(
+            w4_codes[:].rearrange("p (t m b) -> p t m b", t=PACK, b=2),
+            w4_raw[:].rearrange("p (m t b) -> p t m b", t=PACK, b=2),
+        )
+        w4_scale = tile("w4_scale", [P, N], U8)
+        nc.vector.tensor_copy(
+            w4_scale[:].rearrange("p (t m) -> p t m", t=PACK), s4_raw[:].rearrange("p (m t) -> p t m", t=PACK)
+        )
+
+        picked = [tile("picked%d" % h, [P, PACK, HALF], F32) for h in range(HALVES)]
+        for i in range(PACK):
+            for h in range(HALVES):
+                cols = HALF // 16
+                nc.vector.tensor_tensor(
+                    picked[h][:, i, :], planes[i][:].indirect(offsets[:, h * cols : (h + 1) * cols]), wgt_sb[h][:], ALU.mult
+                )
+
+        def weave(copy, dst, src):
+            copy(dst.rearrange("p (c i) t -> p c t i", i=4), src.rearrange("p t (c i) -> p c t i", i=4))
+
+        x_bf = [tile("x_bf%d" % h, [P, HALF, PACK], BF16) for h in range(HALVES)]
+        x_codes = [tile("x_codes%d" % h, [P, HALF], U32) for h in range(HALVES)]
+        x_scale = [tile("x_scale%d" % h, [P, HALF], U8) for h in range(HALVES)]
+
+        def weave_x(h):
+            for c in range(0, HALF, PIECE):
+                weave(nc.scalar.copy, x_bf[h][:, c : c + PIECE, :], picked[h][:, :, c : c + PIECE])
+
+        def quant_x(h):
+            nc.vector.quantize_mx(x_codes[h][:].bitcast(FP8X4), x_scale[h][:], x_bf[h][:].rearrange("p c t -> p (c t)"))
+
+        def deal_weight(copy, w_bf, raw, a):
+            m = WCOLS // PACK
+            copy(
+                w_bf[:].rearrange("p (t m i) -> p m i t", t=PACK, i=PACK)[:, a * m : (a + 1) * m],
+                raw[:].rearrange("p i (m t) -> p m i t", t=PACK),
+            )
+
+        def quant_weight(name, w_bf):
+            codes = tile(name + "_codes", [P, N], U32)
+            scale = tile(name + "_scale", [P, N], U8)
+            for a in range(2):
+                nc.vector.quantize_mx(
+                    codes[:, a * 256 : (a + 1) * 256].bitcast(FP8X4),
+                    scale[:, a * 256 : (a + 1) * 256],
+                    w_bf[:, a * 1024 : (a + 1) * 1024],
+                )
+            return codes, scale
+
+        weave_x(0)
+        wk_bf = tile("wk_bf", [P, PACK * N], BF16)
+        wvd_bf = tile("wvd_bf", [P, PACK * N], BF16)
+        for a in range(2):
+            deal_weight(nc.vector.tensor_copy, wk_bf, wk_raw[a], a)
+        wk_codes, wk_scale = quant_weight("wk", wk_bf)
+        quant_x(0)
+        deal_weight(nc.scalar.copy, wvd_bf, wvd_raw[0], 0)
+        deal_weight(nc.vector.tensor_copy, wvd_bf, wvd_raw[1], 1)
+        wvd_codes, wvd_scale = quant_weight("wvd", wvd_bf)
+
+        gate = [tile("gate%d" % h, [P, PACK, HALF], F32) for h in range(HALVES)]
+        cand = [tile("cand%d" % h, [P, PACK, HALF], F32) for h in range(HALVES)]
+        y = [tile("y%d" % h, [P, PACK, HALF], F32) for h in range(HALVES)]
+        y_bf = [tile("y_bf%d" % h, [P, HALF, PACK], BF16) for h in range(HALVES)]
+        y_codes = tile("y_codes", [P, J], U32)
+        y_scale = tile("y_scale", [P, J], U8)
+        y_rows = out_0.rearrange("(p t) j -> p t j", t=PACK)
+        words = out_1[0].rearrange("p j t -> p (j t)").bitcast(I32)
+
+        def gates(h):
+            for t in range(PACK):
+                cols = slice(t * P, (t + 1) * P)
+                ke = psum.tile([P, HALF], F32, name="ke")
+                nc.tensor.matmul_mx(
+                    ke[:], lhsT=wk_codes[:, cols].bitcast(FP8X4), lhsT_scale=wk_scale[:, cols],
+                    rhs=x_codes[h][:].bitcast(FP8X4), rhs_scale=x_scale[h][:], start=True, stop=True,
+                )
+                nc.scalar.activation(gate[h][:, t, :], ke[:], ACT.Sigmoid, bias=bias[:, t : t + 1])
+
+        def candidates(h):
+            for t in range(PACK):
+                cols = slice(t * P, (t + 1) * P)
+                ve = psum.tile([P, HALF], F32, name="ve")
+                nc.tensor.matmul_mx(
+                    ve[:], lhsT=w4_codes[:, 2 * t * P : 2 * (t + 1) * P].bitcast(FP4X4), lhsT_scale=w4_scale[:, cols],
+                    rhs=x_codes[h][:].bitcast(FP8X4), rhs_scale=x_scale[h][:], start=True, stop=False,
+                )
+                nc.tensor.matmul_mx(
+                    ve[:], lhsT=wvd_codes[:, cols].bitcast(FP8X4), lhsT_scale=wvd_scale[:, cols],
+                    rhs=x_codes[h][:].bitcast(FP8X4), rhs_scale=x_scale[h][:], start=False, stop=True,
+                )
+                nc.scalar.activation(cand[h][:, t, :], ve[:], ACT.Tanh)
+
+        def carry(h):
+            for t in range(PACK):
+                nc.vector.scalar_tensor_tensor(
+                    res_sb[h][:, t, :], gate[h][:, t, :], 1.0, res_sb[h][:, t, :], ALU.subtract, ALU.mult
+                )
+
+        def update(h):
+            for t in range(PACK):
+                nc.vector.tensor_tensor(cand[h][:, t, :], gate[h][:, t, :], cand[h][:, t, :], ALU.mult)
+
+        def pieces(h):
+            c = 0
+            found = []
+            for w in OUT_PIECES[h]:
+                found.append(slice(c, c + w))
+                c = c + w
+            return found
+
+        def mix(h, cols):
+            nc.vector.tensor_tensor(y[h][:, :, cols], cand[h][:, :, cols], res_sb[h][:, :, cols], ALU.subtract)
+            nc.sync.dma_start(y_rows[:, :, h * HALF + cols.start : h * HALF + cols.stop], y[h][:, :, cols])
+
+        def weave_y(copy, h, cols):
+            weave(copy, y_bf[h][:, cols, :], y[h][:, :, cols])
+
+        def quant_y(h, cols):
+            whole = slice(h * HALF + cols.start, h * HALF + cols.stop)
+            nc.vector.quantize_mx(
+                y_codes[:, whole].bitcast(FP8X4), y_scale[:, whole], y_bf[h][:, cols, :].rearrange("p c t -> p (c t)")
+            )
+            nc.sync.dma_start(words[:, whole], y_codes[:, whole].bitcast(I32))
+
+        gates(0)
+        weave_x(1)
+        quant_x(1)
+        candidates(0)
+        carry(0)
+        gates(1)
+        update(0)
+        candidates(1)
+        for cols in pieces(0):
+            mix(0, cols)
+        for cols in pieces(0):
+            weave_y(nc.scalar.copy, 0, cols)
+        carry(1)
+        update(1)
+        for cols in pieces(0):
+            quant_y(0, cols)
+        last = pieces(1)
+        for cols in last:
+            mix(1, cols)
+        for cols in last[:-1]:
+            weave_y(nc.scalar.copy, 1, cols)
+        weave_y(nc.vector.tensor_copy, 1, last[-1])
+        for cols in last:
+            quant_y(1, cols)
+        for q in range(4):
+            queue = nc.sync if q % 2 == 0 else nc.scalar
+            queue.dma_start(
+                out_2[0, 4 * q : 4 * q + 4, :].bitcast(I32), y_scale[32 * q : 32 * q + 4, :].bitcast(I32)
+            )

@@ -1,6 +1,7 @@
 from contextlib import ExitStack
 
 import concourse.mybir as mybir
+from concourse.masks import make_identity
 
 K, N, T, J = 512, 512, 2048, 1024
 FLOPS = 3 * 2 * K * N * J
@@ -22,6 +23,7 @@ HALF = 512
 HALVES = J // HALF
 WCOLS = 256
 PIECE = 256
+FIRST = 256
 OUT_PIECES = ((256, 256), (256, 128, 128))
 
 
@@ -41,31 +43,36 @@ def tile_list_dl_hwaytanhP_kernel(
 
         x_rows = xT.rearrange("(p i) t -> p i t", i=PACK)
         planes = [tile("plane%d" % i, [P, T], F32) for i in range(PACK)]
-        wgt_sb = [tile("wgt%d" % h, [P, HALF], F32) for h in range(HALVES)]
-        nc.sync.dma_start(wgt_sb[0][:], wgt[:, 0:HALF])
-        nc.sync.dma_start(planes[0][:], x_rows[:, 0, :])
-
-        s4_raw = tile("s4_raw", [P, N], U8)
-        nc.gpsimd.memset(s4_raw[:].bitcast(I32), 0)
+        wgt_sb = tile("wgt_sb", [P, J], F32)
+        runs = [slice(a, b) for a, b in ((0, FIRST), (FIRST, HALF), (HALF, J))]
+        ident = tile("ident", [P, P], F32)
+        make_identity(nc, ident[:])
+        wgt_rows = tile("wgt_rows", [P, P], F32)
+        nc.vector.memset(wgt_rows[64:128, :], 0.0)
+        s4_raw = sb.tile([P, N], U8, name="s4_raw", tag="picks", align_bytes=64)
         w4_raw = tile("w4_raw", [P, 2 * N], U8)
-        nc.scalar.dma_start(w4_raw[:].bitcast(I32), wv4_words[0].bitcast(I32))
-        for q in range(4):
-            nc.scalar.dma_start(
-                s4_raw[32 * q : 32 * q + 4, :].bitcast(I32), wv4_scales[0, 4 * q : 4 * q + 4, :].bitcast(I32)
-            )
 
-        nc.sync.dma_start(wgt_sb[1][:], wgt[:, HALF:J])
+        def load_scales(queue, q):
+            rows = wv4_scales[0:1, 4 * q : 4 * q + 4, :].bitcast(I32)
+            queue.dma_start(s4_raw[32 * q : 32 * q + 32, :].bitcast(I32), rows.to_broadcast([8, 4, N // 4]))
+
+        nc.scalar.dma_start(w4_raw[:].bitcast(I32), wv4_words[0].bitcast(I32))
+        for q in range(3):
+            load_scales(nc.scalar, q)
+        load_scales(nc.sync, 3)
+        nc.sync.dma_start(wgt_rows[0:64, :], wgt.rearrange("(g r) (c i) -> g r c i", r=16, i=P)[:, 0])
+        nc.sync.dma_start(planes[0][:], x_rows[:, 0, :])
         for i in range(1, PACK):
             nc.sync.dma_start(planes[i][:], x_rows[:, i, :])
         bias = tile("bias", [P, PACK], F32)
-        nc.sync.dma_start(bias[:], bg.rearrange("(p t) -> p t", t=PACK))
 
         warm = tile("warm", [P, 8], F32)
         nc.vector.memset(warm[:], 0.0)
         nc.scalar.activation(warm[:, 0:1], warm[:, 4:5], ACT.Sigmoid)
 
         def load_weight(name, w, a):
-            raw = tile("%s_raw%d" % (name, a), [P, PACK, WCOLS], F32)
+            tag = "shared" if (name, a) == ("wk", 0) else "%s_raw%d" % (name, a)
+            raw = sb.tile([P, PACK, WCOLS], F32, name="%s_raw%d" % (name, a), tag=tag, align_bytes=64)
             rows = w.rearrange("(p i) c -> p i c", i=PACK)
             nc.sync.dma_start(raw[:], rows[:, :, a * WCOLS : (a + 1) * WCOLS])
             return raw
@@ -77,12 +84,25 @@ def tile_list_dl_hwaytanhP_kernel(
             nc.sync.dma_start(res_sb[h][:, t, :], res_rows[:, t, h * HALF : (h + 1) * HALF])
 
         wk_raw = [load_weight("wk", wk, a) for a in range(2)]
-        load_res(0, 0)
         wvd_raw = [load_weight("wvd", wvd, a) for a in range(2)]
-        for t in range(1, PACK):
-            load_res(0, t)
-        for t in range(PACK):
-            load_res(1, t)
+        nc.sync.dma_start(bias[:], bg.rearrange("(p t) -> p t", t=PACK))
+        for h in range(HALVES):
+            for t in range(PACK):
+                load_res(h, t)
+
+        turned = psum.tile([P, P], F32, name="ve")
+        nc.tensor.transpose(turned[:], wgt_rows[:], ident[:])
+        by_chunk = turned[:, 0:64].rearrange("i (g c) -> i c g", c=8)
+        spread = tile("spread", [P, 8, P], F32)
+        for c in range(0, 8, 2):
+            nc.scalar.copy(
+                spread[:, c : c + 2, :].rearrange("i c (g r) -> i c g r", r=16),
+                by_chunk[:, c : c + 2, :].unsqueeze(3).to_broadcast([P, 2, 8, 16]),
+            )
+            back = psum.tile([P, 2, P], F32, name="ke")
+            for u in range(2):
+                nc.tensor.transpose(back[:, u, :], spread[:, c + u, :], ident[:])
+            nc.scalar.copy(wgt_sb[:, c * P : (c + 2) * P], back[:].rearrange("p u i -> p (u i)"))
 
         w4_codes = tile("w4_codes", [P, 2 * N], U8)
         nc.vector.tensor_copy(
@@ -94,27 +114,34 @@ def tile_list_dl_hwaytanhP_kernel(
             w4_scale[:].rearrange("p (t m) -> p t m", t=PACK), s4_raw[:].rearrange("p (m t) -> p t m", t=PACK)
         )
 
-        picked = [tile("picked%d" % h, [P, PACK, HALF], F32) for h in range(HALVES)]
-        for i in range(PACK):
-            for h in range(HALVES):
-                cols = HALF // 16
-                nc.vector.tensor_tensor(
-                    picked[h][:, i, :], planes[i][:].indirect(offsets[:, h * cols : (h + 1) * cols]), wgt_sb[h][:], ALU.mult
-                )
+        picked = sb.tile([P, PACK, J], F32, name="picked", tag="picks", align_bytes=64)
+        x_codes = [tile("x_codes%d" % h, [P, HALF], U32) for h in range(HALVES)]
+        x_scale = [tile("x_scale%d" % h, [P, HALF], U8) for h in range(HALVES)]
 
         def weave(copy, dst, src):
             copy(dst.rearrange("p (c i) t -> p c t i", i=4), src.rearrange("p t (c i) -> p c t i", i=4))
 
-        x_bf = [tile("x_bf%d" % h, [P, HALF, PACK], BF16) for h in range(HALVES)]
-        x_codes = [tile("x_codes%d" % h, [P, HALF], U32) for h in range(HALVES)]
-        x_scale = [tile("x_scale%d" % h, [P, HALF], U8) for h in range(HALVES)]
+        def gather(i, run):
+            nc.vector.tensor_tensor(
+                picked[:, i, run],
+                planes[i][:].indirect(offsets[:, run.start // 16 : run.stop // 16]),
+                wgt_sb[:, run],
+                ALU.mult,
+            )
 
-        def weave_x(h):
-            for c in range(0, HALF, PIECE):
-                weave(nc.scalar.copy, x_bf[h][:, c : c + PIECE, :], picked[h][:, :, c : c + PIECE])
+        def weave_x(h, copies):
+            x_bf = sb.tile([P, HALF, PACK], BF16, name="x_bf%d" % h, tag="shared", align_bytes=64)
+            for c, copy in zip(range(0, HALF, PIECE), copies):
+                weave(copy, x_bf[:, c : c + PIECE, :], picked[:, :, h * HALF + c : h * HALF + c + PIECE])
+            return x_bf
 
-        def quant_x(h):
-            nc.vector.quantize_mx(x_codes[h][:].bitcast(FP8X4), x_scale[h][:], x_bf[h][:].rearrange("p c t -> p (c t)"))
+        for run in runs:
+            gather(0, run)
+        for i in range(1, PACK - 1):
+            gather(i, slice(0, J))
+
+        def quant_x(h, x_bf):
+            nc.vector.quantize_mx(x_codes[h][:].bitcast(FP8X4), x_scale[h][:], x_bf[:].rearrange("p c t -> p (c t)"))
 
         def deal_weight(copy, w_bf, raw, a):
             m = WCOLS // PACK
@@ -123,27 +150,30 @@ def tile_list_dl_hwaytanhP_kernel(
                 raw[:].rearrange("p i (m t) -> p m i t", t=PACK),
             )
 
-        def quant_weight(name, w_bf):
+        def quant_weight(name, w_bf, calls):
             codes = tile(name + "_codes", [P, N], U32)
             scale = tile(name + "_scale", [P, N], U8)
-            for a in range(2):
+            width = N // calls
+            for c in range(0, N, width):
                 nc.vector.quantize_mx(
-                    codes[:, a * 256 : (a + 1) * 256].bitcast(FP8X4),
-                    scale[:, a * 256 : (a + 1) * 256],
-                    w_bf[:, a * 1024 : (a + 1) * 1024],
+                    codes[:, c : c + width].bitcast(FP8X4), scale[:, c : c + width], w_bf[:, PACK * c : PACK * (c + width)]
                 )
             return codes, scale
 
-        weave_x(0)
         wk_bf = tile("wk_bf", [P, PACK * N], BF16)
         wvd_bf = tile("wvd_bf", [P, PACK * N], BF16)
-        for a in range(2):
-            deal_weight(nc.vector.tensor_copy, wk_bf, wk_raw[a], a)
-        wk_codes, wk_scale = quant_weight("wk", wk_bf)
-        quant_x(0)
-        deal_weight(nc.scalar.copy, wvd_bf, wvd_raw[0], 0)
-        deal_weight(nc.vector.tensor_copy, wvd_bf, wvd_raw[1], 1)
-        wvd_codes, wvd_scale = quant_weight("wvd", wvd_bf)
+        gather(PACK - 1, slice(0, HALF))
+        gather(PACK - 1, slice(HALF, J))
+        deal_weight(nc.scalar.copy, wk_bf, wk_raw[0], 0)
+        deal_weight(nc.vector.tensor_copy, wk_bf, wk_raw[1], 1)
+        x_bf = weave_x(0, (nc.scalar.copy, nc.scalar.copy))
+        wk_codes, wk_scale = quant_weight("wk", wk_bf, 1)
+        deal_weight(nc.vector.tensor_copy, wvd_bf, wvd_raw[0], 0)
+        quant_x(0, x_bf)
+        deal_weight(nc.scalar.copy, wvd_bf, wvd_raw[1], 1)
+        x_bf = weave_x(1, (nc.scalar.copy, nc.vector.tensor_copy))
+        wvd_codes, wvd_scale = quant_weight("wvd", wvd_bf, 1)
+        quant_x(1, x_bf)
 
         gate = [tile("gate%d" % h, [P, PACK, HALF], F32) for h in range(HALVES)]
         cand = [tile("cand%d" % h, [P, PACK, HALF], F32) for h in range(HALVES)]
@@ -178,15 +208,13 @@ def tile_list_dl_hwaytanhP_kernel(
                 )
                 nc.scalar.activation(cand[h][:, t, :], ve[:], ACT.Tanh)
 
-        def carry(h):
-            for t in range(PACK):
-                nc.vector.scalar_tensor_tensor(
-                    res_sb[h][:, t, :], gate[h][:, t, :], 1.0, res_sb[h][:, t, :], ALU.subtract, ALU.mult
-                )
+        def carry(h, ts):
+            nc.vector.scalar_tensor_tensor(
+                res_sb[h][:, ts, :], gate[h][:, ts, :], 1.0, res_sb[h][:, ts, :], ALU.subtract, ALU.mult
+            )
 
-        def update(h):
-            for t in range(PACK):
-                nc.vector.tensor_tensor(cand[h][:, t, :], gate[h][:, t, :], cand[h][:, t, :], ALU.mult)
+        def update(h, ts):
+            nc.vector.tensor_tensor(cand[h][:, ts, :], gate[h][:, ts, :], cand[h][:, ts, :], ALU.mult)
 
         def pieces(h):
             c = 0
@@ -210,30 +238,34 @@ def tile_list_dl_hwaytanhP_kernel(
             )
             nc.sync.dma_start(words[:, whole], y_codes[:, whole].bitcast(I32))
 
+        pairs = (slice(0, 2), slice(2, 4))
+        first, last = pieces(0), pieces(1)
         gates(0)
-        weave_x(1)
-        quant_x(1)
         candidates(0)
-        carry(0)
         gates(1)
-        update(0)
         candidates(1)
-        for cols in pieces(0):
+        for t in range(PACK):
+            carry(0, slice(t, t + 1))
+        for t in range(PACK):
+            update(0, slice(t, t + 1))
+        carry(1, pairs[0])
+        for cols in first:
             mix(0, cols)
-        for cols in pieces(0):
             weave_y(nc.scalar.copy, 0, cols)
-        carry(1)
-        update(1)
-        for cols in pieces(0):
-            quant_y(0, cols)
-        last = pieces(1)
-        for cols in last:
-            mix(1, cols)
-        for cols in last[:-1]:
-            weave_y(nc.scalar.copy, 1, cols)
-        weave_y(nc.vector.tensor_copy, 1, last[-1])
-        for cols in last:
-            quant_y(1, cols)
+        carry(1, pairs[1])
+        update(1, pairs[0])
+        update(1, pairs[1])
+        quant_y(0, first[0])
+        mix(1, last[0])
+        weave_y(nc.scalar.copy, 1, last[0])
+        quant_y(0, first[1])
+        mix(1, last[1])
+        weave_y(nc.scalar.copy, 1, last[1])
+        mix(1, last[2])
+        quant_y(1, last[0])
+        weave_y(nc.vector.tensor_copy, 1, last[2])
+        quant_y(1, last[1])
+        quant_y(1, last[2])
         for q in range(4):
             queue = nc.sync if q % 2 == 0 else nc.scalar
             queue.dma_start(

@@ -39,7 +39,6 @@ def tile_list_dl_hwaytanhP_kernel(
             return sb.tile(shape, dtype, name=name, align_bytes=64)
 
         offsets = sb.tile([P, J // 16], U16, name="offsets")
-        nc.sync.dma_start(offsets[:], offs)
 
         x_rows = xT.rearrange("(p i) t -> p i t", i=PACK)
         planes = [tile("plane%d" % i, [P, T], F32) for i in range(PACK)]
@@ -59,8 +58,9 @@ def tile_list_dl_hwaytanhP_kernel(
         nc.scalar.dma_start(w4_raw[:].bitcast(I32), wv4_words[0].bitcast(I32))
         for q in range(3):
             load_scales(nc.scalar, q)
-        load_scales(nc.sync, 3)
         nc.sync.dma_start(wgt_rows[0:64, :], wgt.rearrange("(g r) (c i) -> g r c i", r=16, i=P)[:, 0])
+        nc.sync.dma_start(offsets[:], offs)
+        load_scales(nc.sync, 3)
         nc.sync.dma_start(planes[0][:], x_rows[:, 0, :])
         for i in range(1, PACK):
             nc.sync.dma_start(planes[i][:], x_rows[:, i, :])
@@ -71,8 +71,7 @@ def tile_list_dl_hwaytanhP_kernel(
         nc.scalar.activation(warm[:, 0:1], warm[:, 4:5], ACT.Sigmoid)
 
         def load_weight(name, w, a):
-            tag = "shared" if (name, a) == ("wk", 0) else "%s_raw%d" % (name, a)
-            raw = sb.tile([P, PACK, WCOLS], F32, name="%s_raw%d" % (name, a), tag=tag, align_bytes=64)
+            raw = sb.tile([P, PACK, WCOLS], F32, name="%s_raw%d" % (name, a), tag="%s_raw%d" % (name, a), align_bytes=64)
             rows = w.rearrange("(p i) c -> p i c", i=PACK)
             nc.sync.dma_start(raw[:], rows[:, :, a * WCOLS : (a + 1) * WCOLS])
             return raw
@@ -115,7 +114,6 @@ def tile_list_dl_hwaytanhP_kernel(
         )
 
         picked = sb.tile([P, PACK, J], F32, name="picked", tag="picks", align_bytes=64)
-        x_codes = [tile("x_codes%d" % h, [P, HALF], U32) for h in range(HALVES)]
         x_scale = [tile("x_scale%d" % h, [P, HALF], U8) for h in range(HALVES)]
 
         def weave(copy, dst, src):
@@ -129,10 +127,9 @@ def tile_list_dl_hwaytanhP_kernel(
                 ALU.mult,
             )
 
-        def weave_x(h, copies):
-            x_bf = sb.tile([P, HALF, PACK], BF16, name="x_bf%d" % h, tag="shared", align_bytes=64)
-            for c, copy in zip(range(0, HALF, PIECE), copies):
-                weave(copy, x_bf[:, c : c + PIECE, :], picked[:, :, h * HALF + c : h * HALF + c + PIECE])
+        def weave_x(copy, cols, tag):
+            x_bf = sb.tile([P, cols.stop - cols.start, PACK], BF16, name="x_bf%d" % cols.start, tag=tag, align_bytes=64)
+            weave(copy, x_bf[:], picked[:, :, cols])
             return x_bf
 
         for run in runs:
@@ -140,8 +137,10 @@ def tile_list_dl_hwaytanhP_kernel(
         for i in range(1, PACK - 1):
             gather(i, slice(0, J))
 
-        def quant_x(h, x_bf):
-            nc.vector.quantize_mx(x_codes[h][:].bitcast(FP8X4), x_scale[h][:], x_bf[:].rearrange("p c t -> p (c t)"))
+        def quant_x(h, cols, x_bf):
+            nc.vector.quantize_mx(
+                x_codes[h][:, cols].bitcast(FP8X4), x_scale[h][:, cols], x_bf[:].rearrange("p c t -> p (c t)")
+            )
 
         def deal_weight(copy, w_bf, raw, a):
             m = WCOLS // PACK
@@ -161,19 +160,23 @@ def tile_list_dl_hwaytanhP_kernel(
             return codes, scale
 
         wk_bf = tile("wk_bf", [P, PACK * N], BF16)
-        wvd_bf = tile("wvd_bf", [P, PACK * N], BF16)
+        wvd_bf = sb.tile([P, PACK * N], BF16, name="wvd_bf", tag="wvd_bf", align_bytes=64)
+        for a in range(2):
+            deal_weight(nc.scalar.copy, wk_bf, wk_raw[a], a)
+        for a in range(2):
+            deal_weight(nc.scalar.copy, wvd_bf, wvd_raw[a], a)
+        x_codes = [tile("x_codes%d" % h, [P, HALF], U32) for h in range(HALVES)]
         gather(PACK - 1, slice(0, HALF))
-        gather(PACK - 1, slice(HALF, J))
-        deal_weight(nc.scalar.copy, wk_bf, wk_raw[0], 0)
-        deal_weight(nc.vector.tensor_copy, wk_bf, wk_raw[1], 1)
-        x_bf = weave_x(0, (nc.scalar.copy, nc.scalar.copy))
+        gather(PACK - 1, slice(HALF, HALF + PIECE))
+        x_bf = weave_x(nc.vector.tensor_copy, slice(0, HALF), "x_bf")
         wk_codes, wk_scale = quant_weight("wk", wk_bf, 1)
-        deal_weight(nc.vector.tensor_copy, wvd_bf, wvd_raw[0], 0)
-        quant_x(0, x_bf)
-        deal_weight(nc.scalar.copy, wvd_bf, wvd_raw[1], 1)
-        x_bf = weave_x(1, (nc.scalar.copy, nc.vector.tensor_copy))
+        quant_x(0, slice(0, HALF), x_bf)
+        gather(PACK - 1, slice(HALF + PIECE, J))
+        x_bf = weave_x(nc.vector.tensor_copy, slice(HALF, HALF + PIECE), "wk_raw1")
+        x_late = weave_x(nc.scalar.copy, slice(HALF + PIECE, J), "wvd_raw1")
         wvd_codes, wvd_scale = quant_weight("wvd", wvd_bf, 1)
-        quant_x(1, x_bf)
+        quant_x(1, slice(0, PIECE), x_bf)
+        quant_x(1, slice(PIECE, HALF), x_late)
 
         gate = [tile("gate%d" % h, [P, PACK, HALF], F32) for h in range(HALVES)]
         cand = [tile("cand%d" % h, [P, PACK, HALF], F32) for h in range(HALVES)]
@@ -198,14 +201,17 @@ def tile_list_dl_hwaytanhP_kernel(
             for t in range(PACK):
                 cols = slice(t * P, (t + 1) * P)
                 ve = psum.tile([P, HALF], F32, name="ve")
-                nc.tensor.matmul_mx(
-                    ve[:], lhsT=w4_codes[:, 2 * t * P : 2 * (t + 1) * P].bitcast(FP4X4), lhsT_scale=w4_scale[:, cols],
-                    rhs=x_codes[h][:].bitcast(FP8X4), rhs_scale=x_scale[h][:], start=True, stop=False,
-                )
-                nc.tensor.matmul_mx(
-                    ve[:], lhsT=wvd_codes[:, cols].bitcast(FP8X4), lhsT_scale=wvd_scale[:, cols],
-                    rhs=x_codes[h][:].bitcast(FP8X4), rhs_scale=x_scale[h][:], start=False, stop=True,
-                )
+                weights = [
+                    (wvd_codes[:, cols].bitcast(FP8X4), wvd_scale[:, cols]),
+                    (w4_codes[:, 2 * t * P : 2 * (t + 1) * P].bitcast(FP4X4), w4_scale[:, cols]),
+                ]
+                if (h, t) == (0, 0):
+                    weights = weights[::-1]
+                for u, (codes, scale) in enumerate(weights):
+                    nc.tensor.matmul_mx(
+                        ve[:], lhsT=codes, lhsT_scale=scale,
+                        rhs=x_codes[h][:].bitcast(FP8X4), rhs_scale=x_scale[h][:], start=u == 0, stop=u == 1,
+                    )
                 nc.scalar.activation(cand[h][:, t, :], ve[:], ACT.Tanh)
 
         def carry(h, ts):
@@ -242,30 +248,28 @@ def tile_list_dl_hwaytanhP_kernel(
         first, last = pieces(0), pieces(1)
         gates(0)
         candidates(0)
-        gates(1)
-        candidates(1)
         for t in range(PACK):
             carry(0, slice(t, t + 1))
         for t in range(PACK):
             update(0, slice(t, t + 1))
-        carry(1, pairs[0])
+        gates(1)
+        candidates(1)
         for cols in first:
             mix(0, cols)
             weave_y(nc.scalar.copy, 0, cols)
+        carry(1, pairs[0])
         carry(1, pairs[1])
         update(1, pairs[0])
         update(1, pairs[1])
-        quant_y(0, first[0])
+        quant_y(0, slice(0, HALF))
         mix(1, last[0])
         weave_y(nc.scalar.copy, 1, last[0])
-        quant_y(0, first[1])
         mix(1, last[1])
         weave_y(nc.scalar.copy, 1, last[1])
         mix(1, last[2])
         quant_y(1, last[0])
         weave_y(nc.vector.tensor_copy, 1, last[2])
-        quant_y(1, last[1])
-        quant_y(1, last[2])
+        quant_y(1, slice(last[1].start, HALF))
         for q in range(4):
             queue = nc.sync if q % 2 == 0 else nc.scalar
             queue.dma_start(

@@ -55,12 +55,12 @@ def tile_list_dl_hwaytanhP_kernel(
             rows = wv4_scales[0:1, 4 * q : 4 * q + 4, :].bitcast(I32)
             queue.dma_start(s4_raw[32 * q : 32 * q + 32, :].bitcast(I32), rows.to_broadcast([8, 4, N // 4]))
 
-        nc.scalar.dma_start(w4_raw[:].bitcast(I32), wv4_words[0].bitcast(I32))
         for q in range(3):
             load_scales(nc.scalar, q)
         nc.sync.dma_start(wgt_rows[0:64, :], wgt.rearrange("(g r) (c i) -> g r c i", r=16, i=P)[:, 0])
         nc.sync.dma_start(offsets[:], offs)
         load_scales(nc.sync, 3)
+        nc.sync.dma_start(w4_raw[:].bitcast(I32), wv4_words[0].bitcast(I32))
         nc.sync.dma_start(planes[0][:], x_rows[:, 0, :])
         for i in range(1, PACK):
             nc.sync.dma_start(planes[i][:], x_rows[:, i, :])
@@ -244,32 +244,94 @@ def tile_list_dl_hwaytanhP_kernel(
             )
             nc.sync.dma_start(words[:, whole], y_codes[:, whole].bitcast(I32))
 
+        blocks = [slice(c, c + P) for c in range(0, PIECE, P)]
+        rest = slice(PIECE, HALF)
+        cand_t = [tile("cand_t%d" % b, [P, PACK, P], F32) for b in range(2)]
+        step_t = [tile("step_t%d" % b, [P, PACK, P], F32) for b in range(2)]
+        w4_all = (w4_codes[:].bitcast(FP4X4), w4_scale[:])
+        wvd_all = (wvd_codes[:].bitcast(FP8X4), wvd_scale[:])
+
+        def flat(ap):
+            return ap.rearrange("p t c -> p (t c)")
+
+        def candidates_turned(b):
+            ve = psum.tile([P, N], F32, name="ve")
+            for u, (codes, scale) in enumerate((wvd_all, w4_all)):
+                nc.tensor.matmul_mx(
+                    ve[:], lhsT=x_codes[1][:, blocks[b]].bitcast(FP8X4), lhsT_scale=x_scale[1][:, blocks[b]],
+                    rhs=codes, rhs_scale=scale, start=u == 0, stop=u == 1,
+                )
+            nc.scalar.activation(flat(cand_t[b][:]), ve[:], ACT.Tanh)
+
+        def turn(src, b, name):
+            bank = psum.tile([P, PACK, P], F32, name=name)
+            for t in range(PACK):
+                nc.tensor.transpose(bank[:, t, :], src[:, t, blocks[b]], ident[:])
+            return bank
+
+        def candidates_rest(ts):
+            ve = psum.tile([P, 2, PIECE], F32, name="ve")
+            for t in range(ts.start, ts.stop):
+                cols = slice(t * P, (t + 1) * P)
+                weights = (
+                    (wvd_codes[:, cols].bitcast(FP8X4), wvd_scale[:, cols]),
+                    (w4_codes[:, 2 * t * P : 2 * (t + 1) * P].bitcast(FP4X4), w4_scale[:, cols]),
+                )
+                for c in range(0, PIECE, P):
+                    places = slice(PIECE + c, PIECE + c + P)
+                    for u, (codes, scale) in enumerate(weights):
+                        nc.tensor.matmul_mx(
+                            ve[:, t - ts.start, c : c + P], lhsT=codes, lhsT_scale=scale,
+                            rhs=x_codes[1][:, places].bitcast(FP8X4), rhs_scale=x_scale[1][:, places],
+                            start=u == 0, stop=u == 1,
+                        )
+            nc.scalar.activation(cand[1][:, ts, rest], ve[:], ACT.Tanh)
+
+        def sum_back(b):
+            bank = psum.tile([P, PACK, P], F32, name="ke")
+            for t in range(PACK):
+                for u, src in enumerate((step_t[b], cand_t[b])):
+                    nc.tensor.matmul(bank[:, t, :], src[:, t, :], ident[:], start=u == 0, stop=u == 1, is_transpose=True)
+            nc.scalar.copy(y[1][:, :, blocks[b]], bank[:])
+
         pairs = (slice(0, 2), slice(2, 4))
-        first, last = pieces(0), pieces(1)
+        first = pieces(0)
+        last = [slice(PIECE, PIECE + P), slice(PIECE + P, HALF)]
         gates(0)
         candidates(0)
         for t in range(PACK):
             carry(0, slice(t, t + 1))
         for t in range(PACK):
             update(0, slice(t, t + 1))
+        for b in range(2):
+            candidates_turned(b)
+        res_t = [turn(res_sb[1], b, "ve") for b in range(2)]
         gates(1)
-        candidates(1)
+        for ts in pairs:
+            candidates_rest(ts)
+        gate_t = [turn(gate[1], b, "ke") for b in range(2)]
         for cols in first:
             mix(0, cols)
             weave_y(nc.scalar.copy, 0, cols)
-        carry(1, pairs[0])
-        carry(1, pairs[1])
-        update(1, pairs[0])
-        update(1, pairs[1])
+        for b in range(2):
+            nc.vector.tensor_tensor(step_t[b][:], cand_t[b][:], res_t[b][:], ALU.subtract)
+        for b in range(2):
+            nc.vector.scalar_tensor_tensor(step_t[b][:], gate_t[b][:], 1.0, step_t[b][:], ALU.subtract, ALU.mult)
+        for b in range(2):
+            sum_back(b)
+        nc.sync.dma_start(y_rows[:, :, HALF : HALF + PIECE], y[1][:, :, 0:PIECE])
+        weave_y(nc.scalar.copy, 1, slice(0, PIECE))
+        nc.vector.scalar_tensor_tensor(
+            res_sb[1][:, :, rest], gate[1][:, :, rest], 1.0, res_sb[1][:, :, rest], ALU.subtract, ALU.mult
+        )
+        nc.vector.tensor_tensor(cand[1][:, :, rest], gate[1][:, :, rest], cand[1][:, :, rest], ALU.mult)
         quant_y(0, slice(0, HALF))
         mix(1, last[0])
         weave_y(nc.scalar.copy, 1, last[0])
         mix(1, last[1])
-        weave_y(nc.scalar.copy, 1, last[1])
-        mix(1, last[2])
-        quant_y(1, last[0])
-        weave_y(nc.vector.tensor_copy, 1, last[2])
-        quant_y(1, slice(last[1].start, HALF))
+        quant_y(1, slice(0, PIECE))
+        weave_y(nc.vector.tensor_copy, 1, last[1])
+        quant_y(1, rest)
         for q in range(4):
             queue = nc.sync if q % 2 == 0 else nc.scalar
             queue.dma_start(

@@ -163,8 +163,7 @@ def tile_list_dl_hwaytanhP_kernel(
         wvd_bf = sb.tile([P, PACK * N], BF16, name="wvd_bf", tag="wvd_bf", align_bytes=64)
         for a in range(2):
             deal_weight(nc.scalar.copy, wk_bf, wk_raw[a], a)
-        for a in range(2):
-            deal_weight(nc.scalar.copy, wvd_bf, wvd_raw[a], a)
+        deal_weight(nc.scalar.copy, wvd_bf, wvd_raw[0], 0)
         x_codes = [tile("x_codes%d" % h, [P, HALF], U32) for h in range(HALVES)]
         gather(PACK - 1, slice(0, HALF))
         gather(PACK - 1, slice(HALF, HALF + PIECE))
@@ -172,11 +171,10 @@ def tile_list_dl_hwaytanhP_kernel(
         wk_codes, wk_scale = quant_weight("wk", wk_bf, 1)
         quant_x(0, slice(0, HALF), x_bf)
         gather(PACK - 1, slice(HALF + PIECE, J))
-        x_bf = weave_x(nc.vector.tensor_copy, slice(HALF, HALF + PIECE), "wk_raw1")
-        x_late = weave_x(nc.scalar.copy, slice(HALF + PIECE, J), "wvd_raw1")
+        deal_weight(nc.vector.tensor_copy, wvd_bf, wvd_raw[1], 1)
+        x_bf = weave_x(nc.vector.tensor_copy, slice(HALF, J), "wk_raw1")
         wvd_codes, wvd_scale = quant_weight("wvd", wvd_bf, 1)
-        quant_x(1, slice(0, PIECE), x_bf)
-        quant_x(1, slice(PIECE, HALF), x_late)
+        quant_x(1, slice(0, HALF), x_bf)
 
         gate = [tile("gate%d" % h, [P, PACK, HALF], F32) for h in range(HALVES)]
         cand = [tile("cand%d" % h, [P, PACK, HALF], F32) for h in range(HALVES)]
@@ -321,14 +319,27 @@ def tile_list_dl_hwaytanhP_kernel(
             sum_back(b)
         nc.sync.dma_start(y_rows[:, :, HALF : HALF + PIECE], y[1][:, :, 0:PIECE])
         weave_y(nc.scalar.copy, 1, slice(0, PIECE))
-        nc.vector.scalar_tensor_tensor(
-            res_sb[1][:, :, rest], gate[1][:, :, rest], 1.0, res_sb[1][:, :, rest], ALU.subtract, ALU.mult
-        )
-        nc.vector.tensor_tensor(cand[1][:, :, rest], gate[1][:, :, rest], cand[1][:, :, rest], ALU.mult)
+
+        def carry_rest(ts):
+            nc.vector.scalar_tensor_tensor(
+                res_sb[1][:, ts, rest], gate[1][:, ts, rest], 1.0, res_sb[1][:, ts, rest], ALU.subtract, ALU.mult
+            )
+
+        def update_rest(ts):
+            nc.vector.tensor_tensor(cand[1][:, ts, rest], gate[1][:, ts, rest], cand[1][:, ts, rest], ALU.mult)
+
+        def mix_rest(ts):
+            nc.vector.tensor_tensor(y[1][:, ts, rest], cand[1][:, ts, rest], res_sb[1][:, ts, rest], ALU.subtract)
+            nc.sync.dma_start(y_rows[:, ts, HALF + PIECE : J], y[1][:, ts, rest])
+
+        carry_rest(pairs[0])
+        update_rest(pairs[0])
+        carry_rest(pairs[1])
+        mix_rest(pairs[0])
+        update_rest(pairs[1])
         quant_y(0, slice(0, HALF))
-        mix(1, last[0])
+        mix_rest(pairs[1])
         weave_y(nc.scalar.copy, 1, last[0])
-        mix(1, last[1])
         quant_y(1, slice(0, PIECE))
         weave_y(nc.vector.tensor_copy, 1, last[1])
         quant_y(1, rest)

@@ -285,12 +285,12 @@ def tile_list_dl_hwaytanhP_kernel(
                         )
             nc.scalar.activation(cand[1][:, ts, rest], ve[:], ACT.Tanh)
 
-        def sum_back(b):
-            bank = psum.tile([P, PACK, P], F32, name="ke")
+        def turn_back(bank, src, opens):
             for t in range(PACK):
-                for u, src in enumerate((step_t[b], cand_t[b])):
-                    nc.tensor.matmul(bank[:, t, :], src[:, t, :], ident[:], start=u == 0, stop=u == 1, is_transpose=True)
-            nc.scalar.copy(y[1][:, :, blocks[b]], bank[:])
+                nc.tensor.matmul(
+                    bank[:, t, :], src[:, t, :], ident[:], is_transpose=True,
+                    start=opens and t == 0, stop=not opens and t == PACK - 1,
+                )
 
         pairs = (slice(0, 2), slice(2, 4))
         first = pieces(0)
@@ -308,17 +308,25 @@ def tile_list_dl_hwaytanhP_kernel(
         for ts in pairs:
             candidates_rest(ts)
         gate_t = [turn(gate[1], b, "ke") for b in range(2)]
-        for cols in first:
-            mix(0, cols)
-            weave_y(nc.scalar.copy, 0, cols)
+        sums = [psum.tile([P, PACK, P], F32, name="ke") for b in range(2)]
+        for b in range(2):
+            turn_back(sums[b], cand_t[b], True)
+        for ts in pairs:
+            nc.vector.tensor_tensor(y[0][:, ts, :], cand[0][:, ts, :], res_sb[0][:, ts, :], ALU.subtract)
+            nc.sync.dma_start(y_rows[:, ts, 0:HALF], y[0][:, ts, :])
+        weave_y(nc.scalar.copy, 0, first[0])
+        nc.gpsimd.tensor_scalar(
+            y_bf[0][:, first[1], :], y[0][:, :, first[1]].rearrange("p t c -> p c t"), 1.0, 0.0, ALU.mult, ALU.add
+        )
         for b in range(2):
             nc.vector.tensor_tensor(step_t[b][:], cand_t[b][:], res_t[b][:], ALU.subtract)
         for b in range(2):
             nc.vector.scalar_tensor_tensor(step_t[b][:], gate_t[b][:], 1.0, step_t[b][:], ALU.subtract, ALU.mult)
         for b in range(2):
-            sum_back(b)
+            turn_back(sums[b], step_t[b], False)
+            nc.scalar.copy(y[1][:, :, blocks[b]], sums[b][:])
+            nc.scalar.copy(y_bf[1][:, blocks[b], :], sums[b][:].rearrange("p t c -> p c t"))
         nc.sync.dma_start(y_rows[:, :, HALF : HALF + PIECE], y[1][:, :, 0:PIECE])
-        weave_y(nc.scalar.copy, 1, slice(0, PIECE))
 
         def carry_rest(ts):
             nc.vector.scalar_tensor_tensor(

@@ -24,7 +24,9 @@ HALVES = J // HALF
 WCOLS = 256
 PIECE = 256
 FIRST = 256
-OUT_PIECES = ((256, 256), (256, 128, 128))
+BLOCKS = J // P
+SUMMED = (4, 5)
+EARLY = 1
 
 
 def tile_list_dl_hwaytanhP_kernel(
@@ -33,23 +35,26 @@ def tile_list_dl_hwaytanhP_kernel(
     nc = tc.nc
     with ExitStack() as ctx:
         sb = ctx.enter_context(tc.tile_pool(name="sb", bufs=1))
-        psum = ctx.enter_context(tc.psum_pool(name="psum", bufs=4))
+        psum = ctx.enter_context(tc.psum_pool(name="psum", bufs=1))
 
-        def tile(name, shape, dtype):
-            return sb.tile(shape, dtype, name=name, align_bytes=64)
+        def tile(name, shape, dtype, tag=None):
+            return sb.tile(shape, dtype, name=name, tag=tag or name, align_bytes=64)
+
+        def bank(n, shape):
+            return psum.tile(shape, F32, name="bank%d" % n)
 
         offsets = sb.tile([P, J // 16], U16, name="offsets")
 
         x_rows = xT.rearrange("(p i) t -> p i t", i=PACK)
         planes = [tile("plane%d" % i, [P, T], F32) for i in range(PACK)]
         wgt_sb = tile("wgt_sb", [P, J], F32)
-        runs = [slice(a, b) for a, b in ((0, FIRST), (FIRST, HALF), (HALF, J))]
         ident = tile("ident", [P, P], F32)
         make_identity(nc, ident[:])
         wgt_rows = tile("wgt_rows", [P, P], F32)
         nc.vector.memset(wgt_rows[64:128, :], 0.0)
-        s4_raw = sb.tile([P, N], U8, name="s4_raw", tag="picks", align_bytes=64)
+        s4_raw = tile("s4_raw", [P, N], U8, "picks")
         w4_raw = tile("w4_raw", [P, 2 * N], U8)
+        bias = tile("bias", [P, PACK], F32)
 
         def load_scales(queue, q):
             rows = wv4_scales[0:1, 4 * q : 4 * q + 4, :].bitcast(I32)
@@ -61,47 +66,43 @@ def tile_list_dl_hwaytanhP_kernel(
         nc.sync.dma_start(offsets[:], offs)
         load_scales(nc.sync, 3)
         nc.sync.dma_start(w4_raw[:].bitcast(I32), wv4_words[0].bitcast(I32))
-        nc.sync.dma_start(planes[0][:], x_rows[:, 0, :])
-        for i in range(1, PACK):
+        for i in range(PACK):
             nc.sync.dma_start(planes[i][:], x_rows[:, i, :])
-        bias = tile("bias", [P, PACK], F32)
 
         warm = tile("warm", [P, 8], F32)
         nc.vector.memset(warm[:], 0.0)
         nc.scalar.activation(warm[:, 0:1], warm[:, 4:5], ACT.Sigmoid)
 
-        def load_weight(name, w, a):
-            raw = sb.tile([P, PACK, WCOLS], F32, name="%s_raw%d" % (name, a), tag="%s_raw%d" % (name, a), align_bytes=64)
+        def load_weight(raw, w, a):
             rows = w.rearrange("(p i) c -> p i c", i=PACK)
-            nc.sync.dma_start(raw[:], rows[:, :, a * WCOLS : (a + 1) * WCOLS])
+            nc.sync.dma_start(raw, rows[:, :, a * WCOLS : (a + 1) * WCOLS])
             return raw
 
         res_rows = res.rearrange("(p t) j -> p t j", t=PACK)
         res_sb = [tile("res%d" % h, [P, PACK, HALF], F32) for h in range(HALVES)]
+        pairs = (slice(0, 2), slice(2, 4))
 
-        def load_res(h, t):
-            nc.sync.dma_start(res_sb[h][:, t, :], res_rows[:, t, h * HALF : (h + 1) * HALF])
-
-        wk_raw = [load_weight("wk", wk, a) for a in range(2)]
-        wvd_raw = [load_weight("wvd", wvd, a) for a in range(2)]
+        wk_raw = [load_weight(tile("wk_raw%d" % a, [P, PACK, WCOLS], F32)[:], wk, a) for a in range(2)]
+        wvd_raw = [load_weight(tile("wvd_raw%d" % a, [P, PACK, WCOLS], F32)[:], wvd, a) for a in range(2)]
         nc.sync.dma_start(bias[:], bg.rearrange("(p t) -> p t", t=PACK))
         for h in range(HALVES):
-            for t in range(PACK):
-                load_res(h, t)
+            for ts in pairs:
+                nc.sync.dma_start(res_sb[h][:, ts, :], res_rows[:, ts, h * HALF : (h + 1) * HALF])
 
-        turned = psum.tile([P, P], F32, name="ve")
+        turned = bank(0, [P, P])
         nc.tensor.transpose(turned[:], wgt_rows[:], ident[:])
         by_chunk = turned[:, 0:64].rearrange("i (g c) -> i c g", c=8)
         spread = tile("spread", [P, 8, P], F32)
         for c in range(0, 8, 2):
-            nc.scalar.copy(
+            copy = nc.scalar.copy
+            copy(
                 spread[:, c : c + 2, :].rearrange("i c (g r) -> i c g r", r=16),
                 by_chunk[:, c : c + 2, :].unsqueeze(3).to_broadcast([P, 2, 8, 16]),
             )
-            back = psum.tile([P, 2, P], F32, name="ke")
+            back = bank(4 + c // 2, [P, 2, P])
             for u in range(2):
                 nc.tensor.transpose(back[:, u, :], spread[:, c + u, :], ident[:])
-            nc.scalar.copy(wgt_sb[:, c * P : (c + 2) * P], back[:].rearrange("p u i -> p (u i)"))
+            copy(wgt_sb[:, c * P : (c + 2) * P], back[:].rearrange("p u i -> p (u i)"))
 
         w4_codes = tile("w4_codes", [P, 2 * N], U8)
         nc.vector.tensor_copy(
@@ -113,8 +114,9 @@ def tile_list_dl_hwaytanhP_kernel(
             w4_scale[:].rearrange("p (t m) -> p t m", t=PACK), s4_raw[:].rearrange("p (m t) -> p t m", t=PACK)
         )
 
-        picked = sb.tile([P, PACK, J], F32, name="picked", tag="picks", align_bytes=64)
         x_scale = [tile("x_scale%d" % h, [P, HALF], U8) for h in range(HALVES)]
+        x_codes = [tile("x_codes%d" % h, [P, HALF], U32) for h in range(HALVES)]
+        picked = tile("picked", [P, PACK, J], F32, "picks")
 
         def weave(copy, dst, src):
             copy(dst.rearrange("p (c i) t -> p c t i", i=4), src.rearrange("p t (c i) -> p c t i", i=4))
@@ -127,110 +129,153 @@ def tile_list_dl_hwaytanhP_kernel(
                 ALU.mult,
             )
 
-        def weave_x(copy, cols, tag):
-            x_bf = sb.tile([P, cols.stop - cols.start, PACK], BF16, name="x_bf%d" % cols.start, tag=tag, align_bytes=64)
-            weave(copy, x_bf[:], picked[:, :, cols])
+        def weave_x(h, tag):
+            x_bf = tile("x_bf%d" % h, [P, HALF, PACK], BF16, tag)
+            weave(nc.vector.tensor_copy, x_bf[:], picked[:, :, h * HALF : (h + 1) * HALF])
             return x_bf
 
-        for run in runs:
-            gather(0, run)
-        for i in range(1, PACK - 1):
-            gather(i, slice(0, J))
-
-        def quant_x(h, cols, x_bf):
-            nc.vector.quantize_mx(
-                x_codes[h][:, cols].bitcast(FP8X4), x_scale[h][:, cols], x_bf[:].rearrange("p c t -> p (c t)")
-            )
+        def quant_x(h, x_bf):
+            nc.vector.quantize_mx(x_codes[h][:].bitcast(FP8X4), x_scale[h][:], x_bf[:].rearrange("p c t -> p (c t)"))
 
         def deal_weight(copy, w_bf, raw, a):
             m = WCOLS // PACK
             copy(
                 w_bf[:].rearrange("p (t m i) -> p m i t", t=PACK, i=PACK)[:, a * m : (a + 1) * m],
-                raw[:].rearrange("p i (m t) -> p m i t", t=PACK),
+                raw.rearrange("p i (m t) -> p m i t", t=PACK),
             )
 
-        def quant_weight(name, w_bf, calls):
+        def quant_weight(name, w_bf):
             codes = tile(name + "_codes", [P, N], U32)
             scale = tile(name + "_scale", [P, N], U8)
-            width = N // calls
-            for c in range(0, N, width):
-                nc.vector.quantize_mx(
-                    codes[:, c : c + width].bitcast(FP8X4), scale[:, c : c + width], w_bf[:, PACK * c : PACK * (c + width)]
-                )
+            nc.vector.quantize_mx(codes[:].bitcast(FP8X4), scale[:], w_bf[:])
             return codes, scale
 
+        for run in (slice(0, FIRST), slice(FIRST, HALF), slice(HALF, J)):
+            gather(0, run)
+        for i in range(1, PACK - 1):
+            gather(i, slice(0, J))
         wk_bf = tile("wk_bf", [P, PACK * N], BF16)
-        wvd_bf = sb.tile([P, PACK * N], BF16, name="wvd_bf", tag="wvd_bf", align_bytes=64)
+        wvd_bf = tile("wvd_bf", [P, PACK * N], BF16)
         for a in range(2):
             deal_weight(nc.scalar.copy, wk_bf, wk_raw[a], a)
         deal_weight(nc.scalar.copy, wvd_bf, wvd_raw[0], 0)
-        x_codes = [tile("x_codes%d" % h, [P, HALF], U32) for h in range(HALVES)]
         gather(PACK - 1, slice(0, HALF))
         gather(PACK - 1, slice(HALF, HALF + PIECE))
-        x_bf = weave_x(nc.vector.tensor_copy, slice(0, HALF), "x_bf")
-        wk_codes, wk_scale = quant_weight("wk", wk_bf, 1)
-        quant_x(0, slice(0, HALF), x_bf)
+        x_bf = weave_x(0, "x_bf")
+        wk_codes, wk_scale = quant_weight("wk", wk_bf)
+        quant_x(0, x_bf)
         gather(PACK - 1, slice(HALF + PIECE, J))
         deal_weight(nc.vector.tensor_copy, wvd_bf, wvd_raw[1], 1)
-        x_bf = weave_x(nc.vector.tensor_copy, slice(HALF, J), "wk_raw1")
-        wvd_codes, wvd_scale = quant_weight("wvd", wvd_bf, 1)
-        quant_x(1, slice(0, HALF), x_bf)
+        x_bf = weave_x(1, "wk_raw1")
+        wvd_codes, wvd_scale = quant_weight("wvd", wvd_bf)
+        quant_x(1, x_bf)
+        less_bias = tile("less_bias", [P, PACK], F32)
+        nc.scalar.activation(less_bias[:], bias[:], ACT.Copy, scale=-1.0)
 
         gate = [tile("gate%d" % h, [P, PACK, HALF], F32) for h in range(HALVES)]
-        cand = [tile("cand%d" % h, [P, PACK, HALF], F32) for h in range(HALVES)]
+        cand_near = tile("cand_near", [P, PACK, HALF], F32)
+        cand = {b: tile("cand%d" % b, [P, PACK, P], F32) for b in SUMMED}
+        cand_rest = tile("cand_rest", [P, PACK, PIECE], F32)
+        step = [tile("step%d" % b, [P, PACK, P], F32) for b in SUMMED]
         y = [tile("y%d" % h, [P, PACK, HALF], F32) for h in range(HALVES)]
         y_bf = [tile("y_bf%d" % h, [P, HALF, PACK], BF16) for h in range(HALVES)]
         y_codes = tile("y_codes", [P, J], U32)
         y_scale = tile("y_scale", [P, J], U8)
         y_rows = out_0.rearrange("(p t) j -> p t j", t=PACK)
         words = out_1[0].rearrange("p j t -> p (j t)").bitcast(I32)
+        w4_all = (w4_codes[:].bitcast(FP4X4), w4_scale[:])
+        wvd_all = (wvd_codes[:].bitcast(FP8X4), wvd_scale[:])
+
+        def places(b):
+            return b // 4, slice(b % 4 * P, (b % 4 + 1) * P)
 
         def gates(h):
             for t in range(PACK):
                 cols = slice(t * P, (t + 1) * P)
-                ke = psum.tile([P, HALF], F32, name="ke")
+                ke = bank(t, [P, HALF])
                 nc.tensor.matmul_mx(
                     ke[:], lhsT=wk_codes[:, cols].bitcast(FP8X4), lhsT_scale=wk_scale[:, cols],
                     rhs=x_codes[h][:].bitcast(FP8X4), rhs_scale=x_scale[h][:], start=True, stop=True,
                 )
-                nc.scalar.activation(gate[h][:, t, :], ke[:], ACT.Sigmoid, bias=bias[:, t : t + 1])
+                if h == 0:
+                    nc.scalar.activation(gate[h][:, t, :], ke[:], ACT.Sigmoid, bias=bias[:, t : t + 1])
+                else:
+                    nc.scalar.activation(
+                        gate[h][:, t, :], ke[:], ACT.Sigmoid, bias=less_bias[:, t : t + 1], scale=-1.0
+                    )
 
-        def candidates(h):
+        def candidates_near():
             for t in range(PACK):
                 cols = slice(t * P, (t + 1) * P)
-                ve = psum.tile([P, HALF], F32, name="ve")
+                ve = bank(4 + t, [P, HALF])
                 weights = [
                     (wvd_codes[:, cols].bitcast(FP8X4), wvd_scale[:, cols]),
                     (w4_codes[:, 2 * t * P : 2 * (t + 1) * P].bitcast(FP4X4), w4_scale[:, cols]),
                 ]
-                if (h, t) == (0, 0):
+                if t < EARLY:
                     weights = weights[::-1]
                 for u, (codes, scale) in enumerate(weights):
                     nc.tensor.matmul_mx(
                         ve[:], lhsT=codes, lhsT_scale=scale,
-                        rhs=x_codes[h][:].bitcast(FP8X4), rhs_scale=x_scale[h][:], start=u == 0, stop=u == 1,
+                        rhs=x_codes[0][:].bitcast(FP8X4), rhs_scale=x_scale[0][:], start=u == 0, stop=u == 1,
                     )
-                nc.scalar.activation(cand[h][:, t, :], ve[:], ACT.Tanh)
+                nc.scalar.activation(cand_near[:, t, :], ve[:], ACT.Tanh)
 
-        def carry(h, ts):
+        def candidates(b, n):
+            h, cols = places(b)
+            ve = bank(n, [P, N])
+            for u, (codes, scale) in enumerate((wvd_all, w4_all)):
+                nc.tensor.matmul_mx(
+                    ve[:], lhsT=x_codes[h][:, cols].bitcast(FP8X4), lhsT_scale=x_scale[h][:, cols],
+                    rhs=codes, rhs_scale=scale, start=u == 0, stop=u == 1,
+                )
+            nc.scalar.activation(cand[b][:], ve[:].rearrange("j (t m) -> j t m", t=PACK), ACT.Tanh)
+
+        def turn(src, n):
+            dst = bank(n, [P, PACK, P])
+            for t in range(PACK):
+                nc.tensor.transpose(dst[:, t, :], src[:, t, :], ident[:])
+            return dst
+
+        def turn_back(dst, src, opens):
+            for t in range(PACK):
+                nc.tensor.matmul(
+                    dst[:, t, :], src[:, t, :], ident[:], is_transpose=True,
+                    start=opens and t == 0, stop=not opens and t == PACK - 1,
+                )
+
+        def carry(dst, h, ts, cols):
             nc.vector.scalar_tensor_tensor(
-                res_sb[h][:, ts, :], gate[h][:, ts, :], 1.0, res_sb[h][:, ts, :], ALU.subtract, ALU.mult
+                dst, gate[h][:, ts, cols], 1.0, res_sb[h][:, ts, cols], ALU.subtract, ALU.mult
             )
 
-        def update(h, ts):
-            nc.vector.tensor_tensor(cand[h][:, ts, :], gate[h][:, ts, :], cand[h][:, ts, :], ALU.mult)
+        def candidates_rest(ts, n):
+            ve = bank(n, [P, 2, PIECE])
+            for t in range(ts.start, ts.stop):
+                cols = slice(t * P, (t + 1) * P)
+                weights = (
+                    (wvd_codes[:, cols].bitcast(FP8X4), wvd_scale[:, cols]),
+                    (w4_codes[:, 2 * t * P : 2 * (t + 1) * P].bitcast(FP4X4), w4_scale[:, cols]),
+                )
+                for c in range(0, PIECE, P):
+                    run = slice(PIECE + c, PIECE + c + P)
+                    for u, (codes, scale) in enumerate(weights):
+                        nc.tensor.matmul_mx(
+                            ve[:, t - ts.start, c : c + P], lhsT=codes, lhsT_scale=scale,
+                            rhs=x_codes[1][:, run].bitcast(FP8X4), rhs_scale=x_scale[1][:, run],
+                            start=u == 0, stop=u == 1,
+                        )
+            nc.scalar.activation(cand_rest[:, ts, :], ve[:], ACT.Tanh)
 
-        def pieces(h):
-            c = 0
-            found = []
-            for w in OUT_PIECES[h]:
-                found.append(slice(c, c + w))
-                c = c + w
-            return found
+        def update(cols):
+            nc.vector.scalar_tensor_tensor(
+                y[1][:, :, cols], gate[1][:, :, cols], 1.0, cand_rest[:, :, cols.start - PIECE : cols.stop - PIECE],
+                ALU.subtract, ALU.mult,
+            )
 
-        def mix(h, cols):
-            nc.vector.tensor_tensor(y[h][:, :, cols], cand[h][:, :, cols], res_sb[h][:, :, cols], ALU.subtract)
-            nc.sync.dma_start(y_rows[:, :, h * HALF + cols.start : h * HALF + cols.stop], y[h][:, :, cols])
+        def mix(h, ts, cols, first, second):
+            nc.vector.tensor_tensor(y[h][:, ts, cols], first, second, ALU.subtract)
+            nc.sync.dma_start(y_rows[:, ts, h * HALF + cols.start : h * HALF + cols.stop], y[h][:, ts, cols])
 
         def weave_y(copy, h, cols):
             weave(copy, y_bf[h][:, cols, :], y[h][:, :, cols])
@@ -240,117 +285,74 @@ def tile_list_dl_hwaytanhP_kernel(
             nc.vector.quantize_mx(
                 y_codes[:, whole].bitcast(FP8X4), y_scale[:, whole], y_bf[h][:, cols, :].rearrange("p c t -> p (c t)")
             )
-            nc.sync.dma_start(words[:, whole], y_codes[:, whole].bitcast(I32))
 
-        blocks = [slice(c, c + P) for c in range(0, PIECE, P)]
-        rest = slice(PIECE, HALF)
-        cand_t = [tile("cand_t%d" % b, [P, PACK, P], F32) for b in range(2)]
-        step_t = [tile("step_t%d" % b, [P, PACK, P], F32) for b in range(2)]
-        w4_all = (w4_codes[:].bitcast(FP4X4), w4_scale[:])
-        wvd_all = (wvd_codes[:].bitcast(FP8X4), wvd_scale[:])
+        def store_words(cols):
+            nc.sync.dma_start(words[:, cols], y_codes[:, cols].bitcast(I32))
 
-        def flat(ap):
-            return ap.rearrange("p t c -> p (t c)")
+        def difference(n):
+            nc.vector.tensor_tensor(step[n][:], res_t[n][:], cand[SUMMED[n]][:], ALU.subtract)
 
-        def candidates_turned(b):
-            ve = psum.tile([P, N], F32, name="ve")
-            for u, (codes, scale) in enumerate((wvd_all, w4_all)):
-                nc.tensor.matmul_mx(
-                    ve[:], lhsT=x_codes[1][:, blocks[b]].bitcast(FP8X4), lhsT_scale=x_scale[1][:, blocks[b]],
-                    rhs=codes, rhs_scale=scale, start=u == 0, stop=u == 1,
-                )
-            nc.scalar.activation(flat(cand_t[b][:]), ve[:], ACT.Tanh)
+        def scaled(n):
+            nc.vector.tensor_tensor(step[n][:], gate_t[n][:], step[n][:], ALU.mult)
+            turn_back(sums[n], step[n], False)
 
-        def turn(src, b, name):
-            bank = psum.tile([P, PACK, P], F32, name=name)
-            for t in range(PACK):
-                nc.tensor.transpose(bank[:, t, :], src[:, t, blocks[b]], ident[:])
-            return bank
+        def leave(n):
+            cols = places(SUMMED[n])[1]
+            nc.scalar.copy(y[1][:, :, cols], sums[n][:])
+            nc.sync.dma_start(y_rows[:, :, HALF + cols.start : HALF + cols.stop], y[1][:, :, cols])
 
-        def candidates_rest(ts):
-            ve = psum.tile([P, 2, PIECE], F32, name="ve")
-            for t in range(ts.start, ts.stop):
-                cols = slice(t * P, (t + 1) * P)
-                weights = (
-                    (wvd_codes[:, cols].bitcast(FP8X4), wvd_scale[:, cols]),
-                    (w4_codes[:, 2 * t * P : 2 * (t + 1) * P].bitcast(FP4X4), w4_scale[:, cols]),
-                )
-                for c in range(0, PIECE, P):
-                    places = slice(PIECE + c, PIECE + c + P)
-                    for u, (codes, scale) in enumerate(weights):
-                        nc.tensor.matmul_mx(
-                            ve[:, t - ts.start, c : c + P], lhsT=codes, lhsT_scale=scale,
-                            rhs=x_codes[1][:, places].bitcast(FP8X4), rhs_scale=x_scale[1][:, places],
-                            start=u == 0, stop=u == 1,
-                        )
-            nc.scalar.activation(cand[1][:, ts, rest], ve[:], ACT.Tanh)
+        def weave_sum(n):
+            nc.scalar.copy(y_bf[1][:, places(SUMMED[n])[1], :], sums[n][:].rearrange("p t c -> p c t"))
 
-        def turn_back(bank, src, opens):
-            for t in range(PACK):
-                nc.tensor.matmul(
-                    bank[:, t, :], src[:, t, :], ident[:], is_transpose=True,
-                    start=opens and t == 0, stop=not opens and t == PACK - 1,
-                )
+        def open_sum(b, n):
+            dst = bank(n, [P, PACK, P])
+            turn_back(dst, cand[b], True)
+            return dst
 
-        pairs = (slice(0, 2), slice(2, 4))
-        first = pieces(0)
-        last = [slice(PIECE, PIECE + P), slice(PIECE + P, HALF)]
+        whole = slice(0, HALF)
+        front, back = slice(0, PIECE), slice(PIECE, HALF)
         gates(0)
-        candidates(0)
+        candidates_near()
         for t in range(PACK):
-            carry(0, slice(t, t + 1))
+            carry(res_sb[0][:, t : t + 1, :], 0, slice(t, t + 1), whole)
         for t in range(PACK):
-            update(0, slice(t, t + 1))
-        for b in range(2):
-            candidates_turned(b)
-        res_t = [turn(res_sb[1], b, "ve") for b in range(2)]
+            nc.vector.tensor_tensor(y[0][:, t, :], cand_near[:, t, :], gate[0][:, t, :], ALU.mult)
         gates(1)
+        for b in SUMMED:
+            candidates(b, b)
+        res_t = [turn(res_sb[1][:, :, places(b)[1]], 2 + b) for b in SUMMED]
+        for n, ts in enumerate(pairs):
+            candidates_rest(ts, n)
+        gate_t = [turn(gate[1][:, :, places(b)[1]], b - 2) for b in SUMMED]
+        sums = [open_sum(b, b) for b in SUMMED]
         for ts in pairs:
-            candidates_rest(ts)
-        gate_t = [turn(gate[1], b, "ke") for b in range(2)]
-        sums = [psum.tile([P, PACK, P], F32, name="ke") for b in range(2)]
-        for b in range(2):
-            turn_back(sums[b], cand_t[b], True)
-        for ts in pairs:
-            nc.vector.tensor_tensor(y[0][:, ts, :], cand[0][:, ts, :], res_sb[0][:, ts, :], ALU.subtract)
-            nc.sync.dma_start(y_rows[:, ts, 0:HALF], y[0][:, ts, :])
-        weave_y(nc.scalar.copy, 0, first[0])
-        nc.gpsimd.tensor_scalar(
-            y_bf[0][:, first[1], :], y[0][:, :, first[1]].rearrange("p t c -> p c t"), 1.0, 0.0, ALU.mult, ALU.add
-        )
-        for b in range(2):
-            nc.vector.tensor_tensor(step_t[b][:], cand_t[b][:], res_t[b][:], ALU.subtract)
-        for b in range(2):
-            nc.vector.scalar_tensor_tensor(step_t[b][:], gate_t[b][:], 1.0, step_t[b][:], ALU.subtract, ALU.mult)
-        for b in range(2):
-            turn_back(sums[b], step_t[b], False)
-            nc.scalar.copy(y[1][:, :, blocks[b]], sums[b][:])
-            nc.scalar.copy(y_bf[1][:, blocks[b], :], sums[b][:].rearrange("p t c -> p c t"))
-        nc.sync.dma_start(y_rows[:, :, HALF : HALF + PIECE], y[1][:, :, 0:PIECE])
-
-        def carry_rest(ts):
-            nc.vector.scalar_tensor_tensor(
-                res_sb[1][:, ts, rest], gate[1][:, ts, rest], 1.0, res_sb[1][:, ts, rest], ALU.subtract, ALU.mult
-            )
-
-        def update_rest(ts):
-            nc.vector.tensor_tensor(cand[1][:, ts, rest], gate[1][:, ts, rest], cand[1][:, ts, rest], ALU.mult)
-
-        def mix_rest(ts):
-            nc.vector.tensor_tensor(y[1][:, ts, rest], cand[1][:, ts, rest], res_sb[1][:, ts, rest], ALU.subtract)
-            nc.sync.dma_start(y_rows[:, ts, HALF + PIECE : J], y[1][:, ts, rest])
-
-        carry_rest(pairs[0])
-        update_rest(pairs[0])
-        carry_rest(pairs[1])
-        mix_rest(pairs[0])
-        update_rest(pairs[1])
-        quant_y(0, slice(0, HALF))
-        mix_rest(pairs[1])
-        weave_y(nc.scalar.copy, 1, last[0])
-        quant_y(1, slice(0, PIECE))
-        weave_y(nc.vector.tensor_copy, 1, last[1])
-        quant_y(1, rest)
+            mix(0, ts, whole, y[0][:, ts, :], res_sb[0][:, ts, :])
+        carried = res_sb[0][:, pairs[1], :].rearrange("p a (b c) -> p (a b) c", b=2)
+        nc.gpsimd.tensor_tensor(carried, gate[1][:, :, back], res_sb[1][:, :, back], ALU.mult)
+        weave_y(nc.scalar.copy, 0, front)
+        difference(0)
+        difference(1)
+        scaled(0)
+        scaled(1)
+        leave(0)
+        leave(1)
+        weave_y(nc.scalar.copy, 0, back)
+        weave_sum(0)
+        weave_sum(1)
+        late = [places(b)[1] for b in (6, 7)]
+        for cols in late:
+            update(cols)
+        quant_y(0, whole)
+        store_words(whole)
+        for cols in late:
+            mix(1, slice(0, PACK), cols, carried[:, :, cols.start - PIECE : cols.stop - PIECE], y[1][:, :, cols])
+        weave_y(nc.scalar.copy, 1, late[0])
+        quant_y(1, front)
+        store_words(slice(HALF, HALF + PIECE))
+        weave_y(nc.vector.tensor_copy, 1, late[1])
+        for cols in late:
+            quant_y(1, cols)
+        store_words(slice(HALF + PIECE, J))
         for q in range(4):
             queue = nc.sync if q % 2 == 0 else nc.scalar
             queue.dma_start(

@@ -129,10 +129,6 @@ def tile_list_dl_hwaytanhP_kernel(
                 ALU.mult,
             )
 
-        def weave_x(h, tag):
-            x_bf = tile("x_bf%d" % h, [P, HALF, PACK], BF16, tag)
-            weave(nc.vector.tensor_copy, x_bf[:], picked[:, :, h * HALF : (h + 1) * HALF])
-            return x_bf
 
         def quant_x(h, x_bf):
             nc.vector.quantize_mx(x_codes[h][:].bitcast(FP8X4), x_scale[h][:], x_bf[:].rearrange("p c t -> p (c t)"))
@@ -152,8 +148,10 @@ def tile_list_dl_hwaytanhP_kernel(
 
         for run in (slice(0, FIRST), slice(FIRST, HALF), slice(HALF, J)):
             gather(0, run)
-        for i in range(1, PACK - 1):
-            gather(i, slice(0, J))
+        gather(1, slice(0, J))
+        x_bf = tile("x_bf0", [P, HALF, PACK], BF16)
+        weave(nc.scalar.copy, x_bf[:, :, 0:2], picked[:, 0:2, 0:HALF])
+        gather(2, slice(0, J))
         wk_bf = tile("wk_bf", [P, PACK * N], BF16)
         wvd_bf = tile("wvd_bf", [P, PACK * N], BF16)
         for a in range(2):
@@ -161,12 +159,13 @@ def tile_list_dl_hwaytanhP_kernel(
         deal_weight(nc.scalar.copy, wvd_bf, wvd_raw[0], 0)
         gather(PACK - 1, slice(0, HALF))
         gather(PACK - 1, slice(HALF, HALF + PIECE))
-        x_bf = weave_x(0, "x_bf")
+        weave(nc.vector.tensor_copy, x_bf[:, :, 2:4], picked[:, 2:4, 0:HALF])
         wk_codes, wk_scale = quant_weight("wk", wk_bf)
         quant_x(0, x_bf)
         gather(PACK - 1, slice(HALF + PIECE, J))
         deal_weight(nc.vector.tensor_copy, wvd_bf, wvd_raw[1], 1)
-        x_bf = weave_x(1, "wk_raw1")
+        x_bf = tile("x_bf1", [P, HALF, PACK], BF16, "wk_raw1")
+        weave(nc.vector.tensor_copy, x_bf[:], picked[:, :, HALF:J])
         wvd_codes, wvd_scale = quant_weight("wvd", wvd_bf)
         quant_x(1, x_bf)
         less_bias = tile("less_bias", [P, PACK], F32)
@@ -178,7 +177,7 @@ def tile_list_dl_hwaytanhP_kernel(
         cand_rest = tile("cand_rest", [P, PACK, PIECE], F32)
         step = [tile("step%d" % b, [P, PACK, P], F32) for b in SUMMED]
         y = [tile("y%d" % h, [P, PACK, HALF], F32) for h in range(HALVES)]
-        y_bf = [tile("y_bf%d" % h, [P, HALF, PACK], BF16) for h in range(HALVES)]
+        y_bf = {c: tile("y_bf%d" % c, [P, PIECE, PACK], BF16) for c in (0, HALF, HALF + PIECE)}
         y_codes = tile("y_codes", [P, J], U32)
         y_scale = tile("y_scale", [P, J], U8)
         y_rows = out_0.rearrange("(p t) j -> p t j", t=PACK)
@@ -277,13 +276,17 @@ def tile_list_dl_hwaytanhP_kernel(
             nc.vector.tensor_tensor(y[h][:, ts, cols], first, second, ALU.subtract)
             nc.sync.dma_start(y_rows[:, ts, h * HALF + cols.start : h * HALF + cols.stop], y[h][:, ts, cols])
 
+        def woven(h, cols):
+            c = cols.start // PIECE * PIECE
+            return y_bf[h * HALF + c][:, cols.start - c : cols.stop - c, :]
+
         def weave_y(copy, h, cols):
-            weave(copy, y_bf[h][:, cols, :], y[h][:, :, cols])
+            weave(copy, woven(h, cols), y[h][:, :, cols])
 
         def quant_y(h, cols):
             whole = slice(h * HALF + cols.start, h * HALF + cols.stop)
             nc.vector.quantize_mx(
-                y_codes[:, whole].bitcast(FP8X4), y_scale[:, whole], y_bf[h][:, cols, :].rearrange("p c t -> p (c t)")
+                y_codes[:, whole].bitcast(FP8X4), y_scale[:, whole], woven(h, cols).rearrange("p c t -> p (c t)")
             )
 
         def store_words(cols):
@@ -302,7 +305,7 @@ def tile_list_dl_hwaytanhP_kernel(
             nc.sync.dma_start(y_rows[:, :, HALF + cols.start : HALF + cols.stop], y[1][:, :, cols])
 
         def weave_sum(n):
-            nc.scalar.copy(y_bf[1][:, places(SUMMED[n])[1], :], sums[n][:].rearrange("p t c -> p c t"))
+            nc.scalar.copy(woven(1, places(SUMMED[n])[1]), sums[n][:].rearrange("p t c -> p c t"))
 
         def open_sum(b, n):
             dst = bank(n, [P, PACK, P])
@@ -336,22 +339,23 @@ def tile_list_dl_hwaytanhP_kernel(
         scaled(1)
         leave(0)
         leave(1)
-        weave_y(nc.scalar.copy, 0, back)
         weave_sum(0)
         weave_sum(1)
         late = [places(b)[1] for b in (6, 7)]
         for cols in late:
             update(cols)
-        quant_y(0, whole)
-        store_words(whole)
+        quant_y(0, front)
+        store_words(front)
         for cols in late:
             mix(1, slice(0, PACK), cols, carried[:, :, cols.start - PIECE : cols.stop - PIECE], y[1][:, :, cols])
+        y_bf[PIECE] = tile("y_bf_back", [P, PIECE, PACK], BF16, "step4")
+        weave_y(nc.vector.tensor_copy, 0, back)
         weave_y(nc.scalar.copy, 1, late[0])
-        quant_y(1, front)
-        store_words(slice(HALF, HALF + PIECE))
         weave_y(nc.vector.tensor_copy, 1, late[1])
-        for cols in late:
-            quant_y(1, cols)
+        quant_y(0, back)
+        quant_y(1, front)
+        store_words(slice(PIECE, HALF + PIECE))
+        quant_y(1, back)
         store_words(slice(HALF + PIECE, J))
         for q in range(4):
             queue = nc.sync if q % 2 == 0 else nc.scalar

@@ -27,6 +27,7 @@ FIRST = 256
 BLOCKS = J // P
 SUMMED = (4, 5)
 EARLY = 1
+SWAPPED = (1, 0, 3, 2)
 
 
 def tile_list_dl_hwaytanhP_kernel(
@@ -189,6 +190,7 @@ def tile_list_dl_hwaytanhP_kernel(
             return b // 4, slice(b % 4 * P, (b % 4 + 1) * P)
 
         def gates(h):
+            banks = []
             for t in range(PACK):
                 cols = slice(t * P, (t + 1) * P)
                 ke = bank(t, [P, HALF])
@@ -196,11 +198,13 @@ def tile_list_dl_hwaytanhP_kernel(
                     ke[:], lhsT=wk_codes[:, cols].bitcast(FP8X4), lhsT_scale=wk_scale[:, cols],
                     rhs=x_codes[h][:].bitcast(FP8X4), rhs_scale=x_scale[h][:], start=True, stop=True,
                 )
+                banks.append(ke)
                 if h == 0:
                     nc.scalar.activation(gate[h][:, t, :], ke[:], ACT.Sigmoid, bias=bias[:, t : t + 1])
-                else:
+            if h == 1:
+                for t in SWAPPED:
                     nc.scalar.activation(
-                        gate[h][:, t, :], ke[:], ACT.Sigmoid, bias=less_bias[:, t : t + 1], scale=-1.0
+                        gate[h][:, t, :], banks[t][:], ACT.Sigmoid, bias=less_bias[:, t : t + 1], scale=-1.0
                     )
 
         def candidates_near():
@@ -274,6 +278,8 @@ def tile_list_dl_hwaytanhP_kernel(
 
         def mix(h, ts, cols, first, second):
             nc.vector.tensor_tensor(y[h][:, ts, cols], first, second, ALU.subtract)
+
+        def store(h, ts, cols):
             nc.sync.dma_start(y_rows[:, ts, h * HALF + cols.start : h * HALF + cols.stop], y[h][:, ts, cols])
 
         def woven(h, cols):
@@ -328,9 +334,12 @@ def tile_list_dl_hwaytanhP_kernel(
             candidates_rest(ts, n)
         gate_t = [turn(gate[1][:, :, places(b)[1]], b - 2) for b in SUMMED]
         sums = [open_sum(b, b) for b in SUMMED]
-        for ts in pairs:
-            mix(0, ts, whole, y[0][:, ts, :], res_sb[0][:, ts, :])
-        carried = res_sb[0][:, pairs[1], :].rearrange("p a (b c) -> p (a b) c", b=2)
+        mix(0, pairs[0], whole, y[0][:, pairs[0], :], res_sb[0][:, pairs[0], :])
+        store(0, pairs[0], whole)
+        for ts, cols in ((slice(2, 3), whole), (slice(3, 4), front), (slice(3, 4), back)):
+            mix(0, ts, cols, y[0][:, ts, cols], res_sb[0][:, ts, cols])
+        store(0, pairs[1], whole)
+        carried = res_sb[0][:, :, front]
         nc.gpsimd.tensor_tensor(carried, gate[1][:, :, back], res_sb[1][:, :, back], ALU.mult)
         weave_y(nc.scalar.copy, 0, front)
         difference(0)
@@ -348,6 +357,7 @@ def tile_list_dl_hwaytanhP_kernel(
         store_words(front)
         for cols in late:
             mix(1, slice(0, PACK), cols, carried[:, :, cols.start - PIECE : cols.stop - PIECE], y[1][:, :, cols])
+            store(1, slice(0, PACK), cols)
         y_bf[PIECE] = tile("y_bf_back", [P, PIECE, PACK], BF16, "step4")
         weave_y(nc.vector.tensor_copy, 0, back)
         weave_y(nc.scalar.copy, 1, late[0])
@@ -358,7 +368,6 @@ def tile_list_dl_hwaytanhP_kernel(
         quant_y(1, back)
         store_words(slice(HALF + PIECE, J))
         for q in range(4):
-            queue = nc.sync if q % 2 == 0 else nc.scalar
-            queue.dma_start(
+            nc.scalar.dma_start(
                 out_2[0, 4 * q : 4 * q + 4, :].bitcast(I32), y_scale[32 * q : 32 * q + 4, :].bitcast(I32)
             )

@@ -137,8 +137,8 @@ def tile_list_dl_hwaytanhP_kernel(
         def deal_weight(copy, w_bf, raw, a):
             m = WCOLS // PACK
             copy(
-                w_bf[:].rearrange("p (t m i) -> p m i t", t=PACK, i=PACK)[:, a * m : (a + 1) * m],
-                raw.rearrange("p i (m t) -> p m i t", t=PACK),
+                w_bf[:].rearrange("p (u t m i) -> p u m i t", u=2, t=2, i=PACK)[:, :, a * m : (a + 1) * m],
+                raw.rearrange("p i (m u t) -> p u m i t", u=2, t=2),
             )
 
         def quant_weight(name, w_bf):
@@ -322,8 +322,8 @@ def tile_list_dl_hwaytanhP_kernel(
         front, back = slice(0, PIECE), slice(PIECE, HALF)
         gates(0)
         candidates_near()
-        for t in range(PACK):
-            carry(res_sb[0][:, t : t + 1, :], 0, slice(t, t + 1), whole)
+        for ts in pairs:
+            carry(res_sb[0][:, ts, :], 0, ts, whole)
         for t in range(PACK):
             nc.vector.tensor_tensor(y[0][:, t, :], cand_near[:, t, :], gate[0][:, t, :], ALU.mult)
         gates(1)
@@ -368,6 +368,7 @@ def tile_list_dl_hwaytanhP_kernel(
         quant_y(1, back)
         store_words(slice(HALF + PIECE, J))
         for q in range(4):
-            nc.scalar.dma_start(
+            queue = nc.sync if q % 2 == 0 else nc.scalar
+            queue.dma_start(
                 out_2[0, 4 * q : 4 * q + 4, :].bitcast(I32), y_scale[32 * q : 32 * q + 4, :].bitcast(I32)
             )

@@ -94,16 +94,17 @@ def tile_list_dl_hwaytanhP_kernel(
         nc.tensor.transpose(turned[:], wgt_rows[:], ident[:])
         by_chunk = turned[:, 0:64].rearrange("i (g c) -> i c g", c=8)
         spread = tile("spread", [P, 8, P], F32)
-        for c in range(0, 8, 2):
-            copy = nc.scalar.copy
+        for c, n in ((0, 2), (2, 2), (4, 4)):
+            copy = nc.scalar.copy if c == 0 else nc.vector.tensor_copy
             copy(
-                spread[:, c : c + 2, :].rearrange("i c (g r) -> i c g r", r=16),
-                by_chunk[:, c : c + 2, :].unsqueeze(3).to_broadcast([P, 2, 8, 16]),
+                spread[:, c : c + n, :].rearrange("i c (g r) -> i c g r", r=16),
+                by_chunk[:, c : c + n, :].unsqueeze(3).to_broadcast([P, n, 8, 16]),
             )
+        for c in range(0, 8, 2):
             back = bank(4 + c // 2, [P, 2, P])
             for u in range(2):
                 nc.tensor.transpose(back[:, u, :], spread[:, c + u, :], ident[:])
-            copy(wgt_sb[:, c * P : (c + 2) * P], back[:].rearrange("p u i -> p (u i)"))
+            nc.scalar.copy(wgt_sb[:, c * P : (c + 2) * P], back[:].rearrange("p u i -> p (u i)"))
 
         w4_codes = tile("w4_codes", [P, 2 * N], U8)
         nc.vector.tensor_copy(
@@ -308,10 +309,9 @@ def tile_list_dl_hwaytanhP_kernel(
         def leave(n):
             cols = places(SUMMED[n])[1]
             nc.scalar.copy(y[1][:, :, cols], sums[n][:])
-            nc.sync.dma_start(y_rows[:, :, HALF + cols.start : HALF + cols.stop], y[1][:, :, cols])
 
         def weave_sum(n):
-            nc.scalar.copy(woven(1, places(SUMMED[n])[1]), sums[n][:].rearrange("p t c -> p c t"))
+            weave(nc.scalar.copy, woven(1, places(SUMMED[n])[1]), sums[n][:])
 
         def open_sum(b, n):
             dst = bank(n, [P, PACK, P])
@@ -346,18 +346,21 @@ def tile_list_dl_hwaytanhP_kernel(
         difference(1)
         scaled(0)
         scaled(1)
+        every = slice(0, PACK)
         leave(0)
+        store(1, every, slice(0, P))
         leave(1)
         weave_sum(0)
         weave_sum(1)
-        late = [places(b)[1] for b in (6, 7)]
+        late = [places(b)[1] for b in (7, 6)]
         for cols in late:
             update(cols)
         quant_y(0, front)
         store_words(front)
         for cols in late:
-            mix(1, slice(0, PACK), cols, carried[:, :, cols.start - PIECE : cols.stop - PIECE], y[1][:, :, cols])
-            store(1, slice(0, PACK), cols)
+            mix(1, every, cols, carried[:, :, cols.start - PIECE : cols.stop - PIECE], y[1][:, :, cols])
+        store(1, every, late[0])
+        store(1, every, slice(P, HALF - P))
         y_bf[PIECE] = tile("y_bf_back", [P, PIECE, PACK], BF16, "step4")
         weave_y(nc.vector.tensor_copy, 0, back)
         weave_y(nc.scalar.copy, 1, late[0])

@@ -355,8 +355,6 @@ def tile_list_dl_hwaytanhP_kernel(
         late = [places(b)[1] for b in (7, 6)]
         for cols in late:
             update(cols)
-        quant_y(0, front)
-        store_words(front)
         for cols in late:
             mix(1, every, cols, carried[:, :, cols.start - PIECE : cols.stop - PIECE], y[1][:, :, cols])
         store(1, every, late[0])
@@ -364,10 +362,12 @@ def tile_list_dl_hwaytanhP_kernel(
         y_bf[PIECE] = tile("y_bf_back", [P, PIECE, PACK], BF16, "step4")
         weave_y(nc.vector.tensor_copy, 0, back)
         weave_y(nc.scalar.copy, 1, late[0])
-        weave_y(nc.vector.tensor_copy, 1, late[1])
+        quant_y(0, front)
         quant_y(0, back)
+        store_words(whole)
+        weave_y(nc.vector.tensor_copy, 1, late[1])
         quant_y(1, front)
-        store_words(slice(PIECE, HALF + PIECE))
+        store_words(slice(HALF, HALF + PIECE))
         quant_y(1, back)
         store_words(slice(HALF + PIECE, J))
         for q in range(4):

@@ -26,7 +26,7 @@ PIECE = 256
 FIRST = 256
 BLOCKS = J // P
 SUMMED = (4, 5)
-EARLY = 1
+EARLY = 2
 SWAPPED = (1, 0, 3, 2)
 
 
@@ -159,12 +159,15 @@ def tile_list_dl_hwaytanhP_kernel(
         for a in range(2):
             deal_weight(nc.scalar.copy, wk_bf, wk_raw[a], a)
         deal_weight(nc.scalar.copy, wvd_bf, wvd_raw[0], 0)
-        gather(PACK - 1, slice(0, HALF))
-        gather(PACK - 1, slice(HALF, HALF + PIECE))
-        weave(nc.vector.tensor_copy, x_bf[:, :, 2:4], picked[:, 2:4, 0:HALF])
+        quarters = [slice(c, c + PIECE) for c in range(0, J, PIECE)]
+        for run in quarters[:2]:
+            gather(PACK - 1, run)
+        for run in quarters[:2]:
+            weave(nc.vector.tensor_copy, x_bf[:, run, 2:4], picked[:, 2:4, run])
         wk_codes, wk_scale = quant_weight("wk", wk_bf)
         quant_x(0, x_bf)
-        gather(PACK - 1, slice(HALF + PIECE, J))
+        for run in quarters[2:]:
+            gather(PACK - 1, run)
         deal_weight(nc.vector.tensor_copy, wvd_bf, wvd_raw[1], 1)
         x_bf = tile("x_bf1", [P, HALF, PACK], BF16, "wk_raw1")
         weave(nc.vector.tensor_copy, x_bf[:], picked[:, :, HALF:J])
@@ -179,7 +182,7 @@ def tile_list_dl_hwaytanhP_kernel(
         cand_rest = tile("cand_rest", [P, PACK, PIECE], F32)
         step = [tile("step%d" % b, [P, PACK, P], F32) for b in SUMMED]
         y = [tile("y%d" % h, [P, PACK, HALF], F32) for h in range(HALVES)]
-        y_bf = {c: tile("y_bf%d" % c, [P, PIECE, PACK], BF16) for c in (0, HALF, HALF + PIECE)}
+        y_bf = {0: tile("y_bf0", [P, HALF - P, PACK], BF16), HALF: tile("y_bf1", [P, HALF, PACK], BF16)}
         y_codes = tile("y_codes", [P, J], U32)
         y_scale = tile("y_scale", [P, J], U8)
         y_rows = out_0.rearrange("(p t) j -> p t j", t=PACK)
@@ -284,8 +287,8 @@ def tile_list_dl_hwaytanhP_kernel(
             nc.sync.dma_start(y_rows[:, ts, h * HALF + cols.start : h * HALF + cols.stop], y[h][:, ts, cols])
 
         def woven(h, cols):
-            c = cols.start // PIECE * PIECE
-            return y_bf[h * HALF + c][:, cols.start - c : cols.stop - c, :]
+            c = max(c for c in y_bf if c <= h * HALF + cols.start)
+            return y_bf[c][:, h * HALF + cols.start - c : h * HALF + cols.stop - c, :]
 
         def weave_y(copy, h, cols):
             weave(copy, woven(h, cols), y[h][:, :, cols])
@@ -302,8 +305,9 @@ def tile_list_dl_hwaytanhP_kernel(
         def difference(n):
             nc.vector.tensor_tensor(step[n][:], res_t[n][:], cand[SUMMED[n]][:], ALU.subtract)
 
-        def scaled(n):
-            nc.vector.tensor_tensor(step[n][:], gate_t[n][:], step[n][:], ALU.mult)
+        def scaled(n, runs):
+            for ts in runs:
+                nc.vector.tensor_tensor(step[n][:, ts, :], gate_t[n][:, ts, :], step[n][:, ts, :], ALU.mult)
             turn_back(sums[n], step[n], False)
 
         def leave(n):
@@ -342,14 +346,16 @@ def tile_list_dl_hwaytanhP_kernel(
         carried = res_sb[0][:, :, front]
         nc.gpsimd.tensor_tensor(carried, gate[1][:, :, back], res_sb[1][:, :, back], ALU.mult)
         weave_y(nc.scalar.copy, 0, front)
+        weave_y(nc.scalar.copy, 0, slice(PIECE, HALF - P))
         difference(0)
         difference(1)
-        scaled(0)
-        scaled(1)
+        scaled(0, pairs)
+        scaled(1, [slice(0, PACK)])
         every = slice(0, PACK)
         leave(0)
         store(1, every, slice(0, P))
         leave(1)
+        store(1, every, slice(P, PIECE))
         weave_sum(0)
         weave_sum(1)
         late = [places(b)[1] for b in (7, 6)]
@@ -357,19 +363,19 @@ def tile_list_dl_hwaytanhP_kernel(
             update(cols)
         for cols in late:
             mix(1, every, cols, carried[:, :, cols.start - PIECE : cols.stop - PIECE], y[1][:, :, cols])
-        store(1, every, late[0])
-        store(1, every, slice(P, HALF - P))
-        y_bf[PIECE] = tile("y_bf_back", [P, PIECE, PACK], BF16, "step4")
-        weave_y(nc.vector.tensor_copy, 0, back)
+        for cols in late:
+            store(1, every, cols)
+        y_bf[HALF - P] = tile("y_bf_back", [P, P, PACK], BF16, "step4")
+        weave_y(nc.vector.tensor_copy, 0, slice(HALF - P, HALF))
         weave_y(nc.scalar.copy, 1, late[0])
         quant_y(0, front)
-        quant_y(0, back)
+        quant_y(0, slice(PIECE, HALF - P))
+        quant_y(0, slice(HALF - P, HALF))
         store_words(whole)
         weave_y(nc.vector.tensor_copy, 1, late[1])
         quant_y(1, front)
-        store_words(slice(HALF, HALF + PIECE))
         quant_y(1, back)
-        store_words(slice(HALF + PIECE, J))
+        store_words(slice(HALF, J))
         for q in range(4):
             queue = nc.sync if q % 2 == 0 else nc.scalar
             queue.dma_start(

@@ -66,8 +66,9 @@ def tile_list_dl_hwaytanhP_kernel(
         nc.sync.dma_start(wgt_rows[0:64, :], wgt.rearrange("(g r) (c i) -> g r c i", r=16, i=P)[:, 0])
         nc.sync.dma_start(offsets[:], offs)
         load_scales(nc.sync, 3)
+        nc.sync.dma_start(planes[0][:], x_rows[:, 0, :])
         nc.sync.dma_start(w4_raw[:].bitcast(I32), wv4_words[0].bitcast(I32))
-        for i in range(PACK):
+        for i in range(1, PACK):
             nc.sync.dma_start(planes[i][:], x_rows[:, i, :])
 
         warm = tile("warm", [P, 8], F32)
@@ -106,10 +107,10 @@ def tile_list_dl_hwaytanhP_kernel(
                 nc.tensor.transpose(back[:, u, :], spread[:, c + u, :], ident[:])
             nc.scalar.copy(wgt_sb[:, c * P : (c + 2) * P], back[:].rearrange("p u i -> p (u i)"))
 
-        w4_codes = tile("w4_codes", [P, 2 * N], U8)
-        nc.vector.tensor_copy(
-            w4_codes[:].rearrange("p (t m b) -> p t m b", t=PACK, b=2),
-            w4_raw[:].rearrange("p (m t b) -> p t m b", t=PACK, b=2),
+        w4_codes = tile("w4_codes", [P, 2 * N], U8, "spread")
+        nc.scalar.copy(
+            w4_codes[:].bitcast(U16).rearrange("p (t m) -> p t m", t=PACK),
+            w4_raw[:].bitcast(U16).rearrange("p (m t) -> p t m", t=PACK),
         )
         w4_scale = tile("w4_scale", [P, N], U8)
         nc.vector.tensor_copy(

@@ -112,7 +112,7 @@ def tile_list_dl_hwaytanhP_kernel(
             w4_codes[:].bitcast(U16).rearrange("p (t m) -> p t m", t=PACK),
             w4_raw[:].bitcast(U16).rearrange("p (m t) -> p t m", t=PACK),
         )
-        w4_scale = tile("w4_scale", [P, N], U8)
+        w4_scale = tile("w4_scale", [P, N], U8, "wgt_rows")
         nc.vector.tensor_copy(
             w4_scale[:].rearrange("p (t m) -> p t m", t=PACK), s4_raw[:].rearrange("p (m t) -> p t m", t=PACK)
         )

@@ -61,11 +61,10 @@ def tile_list_dl_hwaytanhP_kernel(
             rows = wv4_scales[0:1, 4 * q : 4 * q + 4, :].bitcast(I32)
             queue.dma_start(s4_raw[32 * q : 32 * q + 32, :].bitcast(I32), rows.to_broadcast([8, 4, N // 4]))
 
-        for q in range(3):
-            load_scales(nc.scalar, q)
         nc.sync.dma_start(wgt_rows[0:64, :], wgt.rearrange("(g r) (c i) -> g r c i", r=16, i=P)[:, 0])
         nc.sync.dma_start(offsets[:], offs)
-        load_scales(nc.sync, 3)
+        for q in range(4):
+            load_scales(nc.sync, q)
         nc.sync.dma_start(planes[0][:], x_rows[:, 0, :])
         nc.sync.dma_start(w4_raw[:].bitcast(I32), wv4_words[0].bitcast(I32))
         for i in range(1, PACK):

@@ -50,22 +50,23 @@ def tile_list_dl_hwaytanhP_kernel(
         planes = [tile("plane%d" % i, [P, T], F32) for i in range(PACK)]
         wgt_sb = tile("wgt_sb", [P, J], F32)
         ident = tile("ident", [P, P], F32)
+        s4_raw = tile("s4_raw", [P, N], U8)
+        nc.gpsimd.memset(s4_raw[:].bitcast(I32), 0)
         make_identity(nc, ident[:])
         wgt_rows = tile("wgt_rows", [P, P], F32)
         nc.vector.memset(wgt_rows[64:128, :], 0.0)
-        s4_raw = tile("s4_raw", [P, N], U8, "picks")
         w4_raw = tile("w4_raw", [P, 2 * N], U8)
         bias = tile("bias", [P, PACK], F32)
 
         def load_scales(queue, q):
-            rows = wv4_scales[0:1, 4 * q : 4 * q + 4, :].bitcast(I32)
-            queue.dma_start(s4_raw[32 * q : 32 * q + 32, :].bitcast(I32), rows.to_broadcast([8, 4, N // 4]))
+            rows = wv4_scales[0, 4 * q : 4 * q + 4, :].bitcast(I32)
+            queue.dma_start(s4_raw[32 * q : 32 * q + 4, :].bitcast(I32), rows)
 
         nc.sync.dma_start(wgt_rows[0:64, :], wgt.rearrange("(g r) (c i) -> g r c i", r=16, i=P)[:, 0])
         nc.sync.dma_start(offsets[:], offs)
+        nc.sync.dma_start(planes[0][:], x_rows[:, 0, :])
         for q in range(4):
             load_scales(nc.sync, q)
-        nc.sync.dma_start(planes[0][:], x_rows[:, 0, :])
         nc.sync.dma_start(w4_raw[:].bitcast(I32), wv4_words[0].bitcast(I32))
         for i in range(1, PACK):
             nc.sync.dma_start(planes[i][:], x_rows[:, i, :])
@@ -95,8 +96,7 @@ def tile_list_dl_hwaytanhP_kernel(
         by_chunk = turned[:, 0:64].rearrange("i (g c) -> i c g", c=8)
         spread = tile("spread", [P, 8, P], F32)
         for c, n in ((0, 2), (2, 2), (4, 4)):
-            copy = nc.scalar.copy if c == 0 else nc.vector.tensor_copy
-            copy(
+            nc.vector.tensor_copy(
                 spread[:, c : c + n, :].rearrange("i c (g r) -> i c g r", r=16),
                 by_chunk[:, c : c + n, :].unsqueeze(3).to_broadcast([P, n, 8, 16]),
             )
@@ -111,14 +111,9 @@ def tile_list_dl_hwaytanhP_kernel(
             w4_codes[:].bitcast(U16).rearrange("p (t m) -> p t m", t=PACK),
             w4_raw[:].bitcast(U16).rearrange("p (m t) -> p t m", t=PACK),
         )
-        w4_scale = tile("w4_scale", [P, N], U8, "wgt_rows")
-        nc.vector.tensor_copy(
-            w4_scale[:].rearrange("p (t m) -> p t m", t=PACK), s4_raw[:].rearrange("p (m t) -> p t m", t=PACK)
-        )
-
         x_scale = [tile("x_scale%d" % h, [P, HALF], U8) for h in range(HALVES)]
         x_codes = [tile("x_codes%d" % h, [P, HALF], U32) for h in range(HALVES)]
-        picked = tile("picked", [P, PACK, J], F32, "picks")
+        picked = tile("picked", [P, PACK, J], F32)
 
         def weave(copy, dst, src):
             copy(dst.rearrange("p (c i) t -> p c t i", i=4), src.rearrange("p t (c i) -> p c t i", i=4))
@@ -150,6 +145,10 @@ def tile_list_dl_hwaytanhP_kernel(
 
         for run in (slice(0, FIRST), slice(FIRST, HALF), slice(HALF, J)):
             gather(0, run)
+        w4_scale = tile("w4_scale", [P, N], U8, "plane0")
+        nc.vector.tensor_copy(
+            w4_scale[:].rearrange("p (t m) -> p t m", t=PACK), s4_raw[:].rearrange("p (m t) -> p t m", t=PACK)
+        )
         gather(1, slice(0, J))
         x_bf = tile("x_bf0", [P, HALF, PACK], BF16)
         weave(nc.scalar.copy, x_bf[:, :, 0:2], picked[:, 0:2, 0:HALF])

@@ -179,7 +179,7 @@ def tile_list_dl_hwaytanhP_kernel(
         cand_near = tile("cand_near", [P, PACK, HALF], F32)
         cand = {b: tile("cand%d" % b, [P, PACK, P], F32) for b in SUMMED}
         cand_rest = tile("cand_rest", [P, PACK, PIECE], F32)
-        step = [tile("step%d" % b, [P, PACK, P], F32) for b in SUMMED]
+        step = tile("step", [P, 2, PACK, P], F32)
         y = [tile("y%d" % h, [P, PACK, HALF], F32) for h in range(HALVES)]
         y_bf = {0: tile("y_bf0", [P, HALF - P, PACK], BF16), HALF: tile("y_bf1", [P, HALF, PACK], BF16)}
         y_codes = tile("y_codes", [P, J], U32)
@@ -243,11 +243,18 @@ def tile_list_dl_hwaytanhP_kernel(
                 nc.tensor.transpose(dst[:, t, :], src[:, t, :], ident[:])
             return dst
 
-        def turn_back(dst, src, opens):
-            for t in range(PACK):
+        def turn_pair(src, ts, n):
+            dst = bank(n, [P, 2, 2, P])
+            for u in range(2):
+                for t in range(ts.start, ts.stop):
+                    nc.tensor.transpose(dst[:, u, t - ts.start, :], src[:, t, u * P : (u + 1) * P], ident[:])
+            return dst
+
+        def turn_back(dst, src, ts, u, opens):
+            for t in range(ts.start, ts.stop):
                 nc.tensor.matmul(
-                    dst[:, t, :], src[:, t, :], ident[:], is_transpose=True,
-                    start=opens and t == 0, stop=not opens and t == PACK - 1,
+                    dst[:, t - ts.start, u * P : (u + 1) * P], src[:, t, :], ident[:], is_transpose=True,
+                    start=opens and u == 0 and t == ts.start, stop=not opens and u == 1 and t == ts.stop - 1,
                 )
 
         def carry(dst, h, ts, cols):
@@ -273,10 +280,9 @@ def tile_list_dl_hwaytanhP_kernel(
                         )
             nc.scalar.activation(cand_rest[:, ts, :], ve[:], ACT.Tanh)
 
-        def update(cols):
+        def update(ts):
             nc.vector.scalar_tensor_tensor(
-                y[1][:, :, cols], gate[1][:, :, cols], 1.0, cand_rest[:, :, cols.start - PIECE : cols.stop - PIECE],
-                ALU.subtract, ALU.mult,
+                y[1][:, ts, back], gate[1][:, ts, back], 1.0, cand_rest[:, ts, :], ALU.subtract, ALU.mult
             )
 
         def mix(h, ts, cols, first, second):
@@ -302,23 +308,23 @@ def tile_list_dl_hwaytanhP_kernel(
             nc.sync.dma_start(words[:, cols], y_codes[:, cols].bitcast(I32))
 
         def difference(n):
-            nc.vector.tensor_tensor(step[n][:], res_t[n][:], cand[SUMMED[n]][:], ALU.subtract)
+            nc.vector.tensor_tensor(step[:, n], res_t[n][:], cand[SUMMED[n]][:], ALU.subtract)
 
         def scaled(n, runs):
-            for ts in runs:
-                nc.vector.tensor_tensor(step[n][:, ts, :], gate_t[n][:, ts, :], step[n][:, ts, :], ALU.mult)
-            turn_back(sums[n], step[n], False)
+            ts = pairs[n]
+            for us in runs:
+                nc.vector.tensor_tensor(step[:, us, ts, :], gate_t[n][:, us], step[:, us, ts, :], ALU.mult)
+                for u in range(us.start, us.stop):
+                    turn_back(sums[n], step[:, u], ts, u, False)
 
         def leave(n):
-            cols = places(SUMMED[n])[1]
-            nc.scalar.copy(y[1][:, :, cols], sums[n][:])
+            nc.scalar.copy(y[1][:, pairs[n], front], sums[n][:])
+            store(1, pairs[n], front)
 
-        def weave_sum(n):
-            weave(nc.scalar.copy, woven(1, places(SUMMED[n])[1]), sums[n][:])
-
-        def open_sum(b, n):
-            dst = bank(n, [P, PACK, P])
-            turn_back(dst, cand[b], True)
+        def open_sum(n):
+            dst = bank(SUMMED[n], [P, 2, PIECE])
+            for u in range(2):
+                turn_back(dst, cand[SUMMED[u]], pairs[n], u, True)
             return dst
 
         whole = slice(0, HALF)
@@ -335,8 +341,8 @@ def tile_list_dl_hwaytanhP_kernel(
         res_t = [turn(res_sb[1][:, :, places(b)[1]], 2 + b) for b in SUMMED]
         for n, ts in enumerate(pairs):
             candidates_rest(ts, n)
-        gate_t = [turn(gate[1][:, :, places(b)[1]], b - 2) for b in SUMMED]
-        sums = [open_sum(b, b) for b in SUMMED]
+        gate_t = [turn_pair(gate[1][:, :, front], ts, 2 + n) for n, ts in enumerate(pairs)]
+        sums = [open_sum(n) for n in range(2)]
         mix(0, pairs[0], whole, y[0][:, pairs[0], :], res_sb[0][:, pairs[0], :])
         store(0, pairs[0], whole)
         for ts, cols in ((slice(2, 3), whole), (slice(3, 4), front), (slice(3, 4), back)):
@@ -348,23 +354,20 @@ def tile_list_dl_hwaytanhP_kernel(
         weave_y(nc.scalar.copy, 0, slice(PIECE, HALF - P))
         difference(0)
         difference(1)
-        scaled(0, pairs)
-        scaled(1, [slice(0, PACK)])
-        every = slice(0, PACK)
+        scaled(0, [slice(0, 1), slice(1, 2)])
+        scaled(1, [slice(0, 2)])
         leave(0)
-        store(1, every, slice(0, P))
         leave(1)
-        store(1, every, slice(P, PIECE))
-        weave_sum(0)
-        weave_sum(1)
+        for b in SUMMED:
+            weave_y(nc.scalar.copy, 1, places(b)[1])
         late = [places(b)[1] for b in (7, 6)]
-        for cols in late:
-            update(cols)
-        for cols in late:
-            mix(1, every, cols, carried[:, :, cols.start - PIECE : cols.stop - PIECE], y[1][:, :, cols])
-        for cols in late:
-            store(1, every, cols)
-        y_bf[HALF - P] = tile("y_bf_back", [P, P, PACK], BF16, "step4")
+        for ts in pairs:
+            update(ts)
+        for ts in pairs:
+            mix(1, ts, back, carried[:, ts, :], y[1][:, ts, back])
+        for ts in pairs:
+            store(1, ts, back)
+        y_bf[HALF - P] = tile("y_bf_back", [P, P, PACK], BF16, "step")
         weave_y(nc.vector.tensor_copy, 0, slice(HALF - P, HALF))
         weave_y(nc.scalar.copy, 1, late[0])
         quant_y(0, front)

@@ -27,6 +27,7 @@ FIRST = 256
 BLOCKS = J // P
 SUMMED = (4, 5)
 EARLY = 2
+SHARE = 32
 SWAPPED = (1, 0, 3, 2)
 
 
@@ -130,11 +131,11 @@ def tile_list_dl_hwaytanhP_kernel(
         def quant_x(h, x_bf):
             nc.vector.quantize_mx(x_codes[h][:].bitcast(FP8X4), x_scale[h][:], x_bf[:].rearrange("p c t -> p (c t)"))
 
-        def deal_weight(copy, w_bf, raw, a):
-            m = WCOLS // PACK
+        def deal_weight(copy, w_bf, raw, a, part=slice(0, WCOLS // PACK)):
+            m = a * WCOLS // PACK
             copy(
-                w_bf[:].rearrange("p (u t m i) -> p u m i t", u=2, t=2, i=PACK)[:, :, a * m : (a + 1) * m],
-                raw.rearrange("p i (m u t) -> p u m i t", u=2, t=2),
+                w_bf[:].rearrange("p (u t m i) -> p u m i t", u=2, t=2, i=PACK)[:, :, m + part.start : m + part.stop],
+                raw.rearrange("p i (m u t) -> p u m i t", u=2, t=2)[:, :, part],
             )
 
         def quant_weight(name, w_bf):
@@ -158,6 +159,7 @@ def tile_list_dl_hwaytanhP_kernel(
         for a in range(2):
             deal_weight(nc.scalar.copy, wk_bf, wk_raw[a], a)
         deal_weight(nc.scalar.copy, wvd_bf, wvd_raw[0], 0)
+        deal_weight(nc.scalar.copy, wvd_bf, wvd_raw[1], 1, slice(0, SHARE))
         quarters = [slice(c, c + PIECE) for c in range(0, J, PIECE)]
         for run in quarters[:2]:
             gather(PACK - 1, run)
@@ -167,7 +169,7 @@ def tile_list_dl_hwaytanhP_kernel(
         quant_x(0, x_bf)
         for run in quarters[2:]:
             gather(PACK - 1, run)
-        deal_weight(nc.vector.tensor_copy, wvd_bf, wvd_raw[1], 1)
+        deal_weight(nc.vector.tensor_copy, wvd_bf, wvd_raw[1], 1, slice(SHARE, WCOLS // PACK))
         x_bf = tile("x_bf1", [P, HALF, PACK], BF16, "wk_raw1")
         weave(nc.vector.tensor_copy, x_bf[:], picked[:, :, HALF:J])
         wvd_codes, wvd_scale = quant_weight("wvd", wvd_bf)

@@ -381,7 +381,7 @@ def tile_list_dl_hwaytanhP_kernel(
         quant_y(1, back)
         store_words(slice(HALF, J))
         for q in range(4):
-            queue = nc.sync if q % 2 == 0 else nc.scalar
+            queue = nc.sync if q == 0 else nc.scalar
             queue.dma_start(
                 out_2[0, 4 * q : 4 * q + 4, :].bitcast(I32), y_scale[32 * q : 32 * q + 4, :].bitcast(I32)
             )

from contextlib import ExitStack

import concourse.mybir as mybir
from concourse.masks import make_identity

K, N, T, J = 512, 512, 2048, 1024
FLOPS = 3 * 2 * K * N * J

F32 = mybir.dt.float32
BF16 = mybir.dt.bfloat16
I32 = mybir.dt.int32
U32 = mybir.dt.uint32
U16 = mybir.dt.uint16
U8 = mybir.dt.uint8
FP8X4 = mybir.dt.float8_e4m3fn_x4
FP4X4 = mybir.dt.float4_e2m1fn_x4
ALU = mybir.AluOpType
ACT = mybir.ActivationFunctionType

P = 128
PACK = 4
HALF = 512
HALVES = J // HALF
WCOLS = 256
PIECE = 256
FIRST = 256
BLOCKS = J // P
SUMMED = (4, 5)
EARLY = 2
SHARE = 32
SWAPPED = (1, 0, 3, 2)


def tile_list_dl_hwaytanhP_kernel(
    tc, xT, wgt, wk, wv4_words, wv4_scales, wvd, bg, res, offs, out_0, out_1, out_2
):
    nc = tc.nc
    with ExitStack() as ctx:
        sb = ctx.enter_context(tc.tile_pool(name="sb", bufs=1))
        psum = ctx.enter_context(tc.psum_pool(name="psum", bufs=1))

        def tile(name, shape, dtype, tag=None):
            return sb.tile(shape, dtype, name=name, tag=tag or name, align_bytes=64)

        def bank(n, shape):
            return psum.tile(shape, F32, name="bank%d" % n)

        offsets = sb.tile([P, J // 16], U16, name="offsets")

        x_rows = xT.rearrange("(p i) t -> p i t", i=PACK)
        planes = [tile("plane%d" % i, [P, T], F32) for i in range(PACK)]
        wgt_sb = tile("wgt_sb", [P, J], F32)
        ident = tile("ident", [P, P], F32)
        s4_raw = tile("s4_raw", [P, N], U8)
        nc.gpsimd.memset(s4_raw[:].bitcast(I32), 0)
        make_identity(nc, ident[:])
        wgt_rows = tile("wgt_rows", [P, P], F32)
        nc.vector.memset(wgt_rows[64:128, :], 0.0)
        w4_raw = tile("w4_raw", [P, 2 * N], U8)
        bias = tile("bias", [P, PACK], F32)

        def load_scales(queue, q):
            rows = wv4_scales[0, 4 * q : 4 * q + 4, :].bitcast(I32)
            queue.dma_start(s4_raw[32 * q : 32 * q + 4, :].bitcast(I32), rows)

        nc.sync.dma_start(wgt_rows[0:64, :], wgt.rearrange("(g r) (c i) -> g r c i", r=16, i=P)[:, 0])
        nc.sync.dma_start(offsets[:], offs)
        nc.sync.dma_start(planes[0][:], x_rows[:, 0, :])
        for q in range(4):
            load_scales(nc.sync, q)
        nc.sync.dma_start(w4_raw[:].bitcast(I32), wv4_words[0].bitcast(I32))
        for i in range(1, PACK):
            nc.sync.dma_start(planes[i][:], x_rows[:, i, :])

        warm = tile("warm", [P, 8], F32)
        nc.vector.memset(warm[:], 0.0)
        nc.scalar.activation(warm[:, 0:1], warm[:, 4:5], ACT.Sigmoid)

        def load_weight(raw, w, a):
            rows = w.rearrange("(p i) c -> p i c", i=PACK)
            nc.sync.dma_start(raw, rows[:, :, a * WCOLS : (a + 1) * WCOLS])
            return raw

        res_rows = res.rearrange("(p t) j -> p t j", t=PACK)
        res_sb = [tile("res%d" % h, [P, PACK, HALF], F32) for h in range(HALVES)]
        pairs = (slice(0, 2), slice(2, 4))

        wk_raw = [load_weight(tile("wk_raw%d" % a, [P, PACK, WCOLS], F32)[:], wk, a) for a in range(2)]
        wvd_raw = [load_weight(tile("wvd_raw%d" % a, [P, PACK, WCOLS], F32)[:], wvd, a) for a in range(2)]
        nc.sync.dma_start(bias[:], bg.rearrange("(p t) -> p t", t=PACK))
        for h in range(HALVES):
            for ts in pairs:
                nc.sync.dma_start(res_sb[h][:, ts, :], res_rows[:, ts, h * HALF : (h + 1) * HALF])

        turned = bank(0, [P, P])
        nc.tensor.transpose(turned[:], wgt_rows[:], ident[:])
        by_chunk = turned[:, 0:64].rearrange("i (g c) -> i c g", c=8)
        spread = tile("spread", [P, 8, P], F32)
        for c, n in ((0, 2), (2, 2), (4, 4)):
            nc.vector.tensor_copy(
                spread[:, c : c + n, :].rearrange("i c (g r) -> i c g r", r=16),
                by_chunk[:, c : c + n, :].unsqueeze(3).to_broadcast([P, n, 8, 16]),
            )
        for c in range(0, 8, 2):
            back = bank(4 + c // 2, [P, 2, P])
            for u in range(2):
                nc.tensor.transpose(back[:, u, :], spread[:, c + u, :], ident[:])
            nc.scalar.copy(wgt_sb[:, c * P : (c + 2) * P], back[:].rearrange("p u i -> p (u i)"))

        w4_codes = tile("w4_codes", [P, 2 * N], U8, "spread")
        nc.scalar.copy(
            w4_codes[:].bitcast(U16).rearrange("p (t m) -> p t m", t=PACK),
            w4_raw[:].bitcast(U16).rearrange("p (m t) -> p t m", t=PACK),
        )
        x_scale = [tile("x_scale%d" % h, [P, HALF], U8) for h in range(HALVES)]
        x_codes = [tile("x_codes%d" % h, [P, HALF], U32) for h in range(HALVES)]
        picked = tile("picked", [P, PACK, J], F32)

        def weave(copy, dst, src):
            copy(dst.rearrange("p (c i) t -> p c t i", i=4), src.rearrange("p t (c i) -> p c t i", i=4))

        def gather(i, run):
            nc.vector.tensor_tensor(
                picked[:, i, run],
                planes[i][:].indirect(offsets[:, run.start // 16 : run.stop // 16]),
                wgt_sb[:, run],
                ALU.mult,
            )


        def quant_x(h, x_bf):
            nc.vector.quantize_mx(x_codes[h][:].bitcast(FP8X4), x_scale[h][:], x_bf[:].rearrange("p c t -> p (c t)"))

        def deal_weight(copy, w_bf, raw, a, part=slice(0, WCOLS // PACK)):
            m = a * WCOLS // PACK
            copy(
                w_bf[:].rearrange("p (u t m i) -> p u m i t", u=2, t=2, i=PACK)[:, :, m + part.start : m + part.stop],
                raw.rearrange("p i (m u t) -> p u m i t", u=2, t=2)[:, :, part],
            )

        def quant_weight(name, w_bf):
            codes = tile(name + "_codes", [P, N], U32)
            scale = tile(name + "_scale", [P, N], U8)
            nc.vector.quantize_mx(codes[:].bitcast(FP8X4), scale[:], w_bf[:])
            return codes, scale

        for run in (slice(0, FIRST), slice(FIRST, HALF), slice(HALF, J)):
            gather(0, run)
        w4_scale = tile("w4_scale", [P, N], U8, "plane0")
        nc.vector.tensor_copy(
            w4_scale[:].rearrange("p (t m) -> p t m", t=PACK), s4_raw[:].rearrange("p (m t) -> p t m", t=PACK)
        )
        gather(1, slice(0, J))
        x_bf = tile("x_bf0", [P, HALF, PACK], BF16)
        weave(nc.scalar.copy, x_bf[:, :, 0:2], picked[:, 0:2, 0:HALF])
        gather(2, slice(0, J))
        wk_bf = tile("wk_bf", [P, PACK * N], BF16)
        wvd_bf = tile("wvd_bf", [P, PACK * N], BF16)
        for a in range(2):
            deal_weight(nc.scalar.copy, wk_bf, wk_raw[a], a)
        deal_weight(nc.scalar.copy, wvd_bf, wvd_raw[0], 0)
        deal_weight(nc.scalar.copy, wvd_bf, wvd_raw[1], 1, slice(0, SHARE))
        quarters = [slice(c, c + PIECE) for c in range(0, J, PIECE)]
        for run in quarters[:2]:
            gather(PACK - 1, run)
        for run in quarters[:2]:
            weave(nc.vector.tensor_copy, x_bf[:, run, 2:4], picked[:, 2:4, run])
        wk_codes, wk_scale = quant_weight("wk", wk_bf)
        quant_x(0, x_bf)
        for run in quarters[2:]:
            gather(PACK - 1, run)
        deal_weight(nc.vector.tensor_copy, wvd_bf, wvd_raw[1], 1, slice(SHARE, WCOLS // PACK))
        x_bf = tile("x_bf1", [P, HALF, PACK], BF16, "wk_raw1")
        weave(nc.vector.tensor_copy, x_bf[:], picked[:, :, HALF:J])
        wvd_codes, wvd_scale = quant_weight("wvd", wvd_bf)
        quant_x(1, x_bf)
        less_bias = tile("less_bias", [P, PACK], F32)
        nc.scalar.activation(less_bias[:], bias[:], ACT.Copy, scale=-1.0)

        gate = [tile("gate%d" % h, [P, PACK, HALF], F32) for h in range(HALVES)]
        cand_near = tile("cand_near", [P, PACK, HALF], F32)
        cand = {b: tile("cand%d" % b, [P, PACK, P], F32) for b in SUMMED}
        cand_rest = tile("cand_rest", [P, PACK, PIECE], F32)
        step = tile("step", [P, 2, PACK, P], F32)
        y = [tile("y%d" % h, [P, PACK, HALF], F32) for h in range(HALVES)]
        y_bf = {0: tile("y_bf0", [P, HALF - P, PACK], BF16), HALF: tile("y_bf1", [P, HALF, PACK], BF16)}
        y_codes = tile("y_codes", [P, J], U32)
        y_scale = tile("y_scale", [P, J], U8)
        y_rows = out_0.rearrange("(p t) j -> p t j", t=PACK)
        words = out_1[0].rearrange("p j t -> p (j t)").bitcast(I32)
        w4_all = (w4_codes[:].bitcast(FP4X4), w4_scale[:])
        wvd_all = (wvd_codes[:].bitcast(FP8X4), wvd_scale[:])

        def places(b):
            return b // 4, slice(b % 4 * P, (b % 4 + 1) * P)

        def gates(h):
            banks = []
            for t in range(PACK):
                cols = slice(t * P, (t + 1) * P)
                ke = bank(t, [P, HALF])
                nc.tensor.matmul_mx(
                    ke[:], lhsT=wk_codes[:, cols].bitcast(FP8X4), lhsT_scale=wk_scale[:, cols],
                    rhs=x_codes[h][:].bitcast(FP8X4), rhs_scale=x_scale[h][:], start=True, stop=True,
                )
                banks.append(ke)
                if h == 0:
                    nc.scalar.activation(gate[h][:, t, :], ke[:], ACT.Sigmoid, bias=bias[:, t : t + 1])
            if h == 1:
                for t in SWAPPED:
                    nc.scalar.activation(
                        gate[h][:, t, :], banks[t][:], ACT.Sigmoid, bias=less_bias[:, t : t + 1], scale=-1.0
                    )

        def candidates_near():
            for t in range(PACK):
                cols = slice(t * P, (t + 1) * P)
                ve = bank(4 + t, [P, HALF])
                weights = [
                    (wvd_codes[:, cols].bitcast(FP8X4), wvd_scale[:, cols]),
                    (w4_codes[:, 2 * t * P : 2 * (t + 1) * P].bitcast(FP4X4), w4_scale[:, cols]),
                ]
                if t < EARLY:
                    weights = weights[::-1]
                for u, (codes, scale) in enumerate(weights):
                    nc.tensor.matmul_mx(
                        ve[:], lhsT=codes, lhsT_scale=scale,
                        rhs=x_codes[0][:].bitcast(FP8X4), rhs_scale=x_scale[0][:], start=u == 0, stop=u == 1,
                    )
                nc.scalar.activation(cand_near[:, t, :], ve[:], ACT.Tanh)

        def candidates(b, n):
            h, cols = places(b)
            ve = bank(n, [P, N])
            for u, (codes, scale) in enumerate((wvd_all, w4_all)):
                nc.tensor.matmul_mx(
                    ve[:], lhsT=x_codes[h][:, cols].bitcast(FP8X4), lhsT_scale=x_scale[h][:, cols],
                    rhs=codes, rhs_scale=scale, start=u == 0, stop=u == 1,
                )
            nc.scalar.activation(cand[b][:], ve[:].rearrange("j (t m) -> j t m", t=PACK), ACT.Tanh)

        def turn(src, n):
            dst = bank(n, [P, PACK, P])
            for t in range(PACK):
                nc.tensor.transpose(dst[:, t, :], src[:, t, :], ident[:])
            return dst

        def turn_pair(src, ts, n):
            dst = bank(n, [P, 2, 2, P])
            for u in range(2):
                for t in range(ts.start, ts.stop):
                    nc.tensor.transpose(dst[:, u, t - ts.start, :], src[:, t, u * P : (u + 1) * P], ident[:])
            return dst

        def turn_back(dst, src, ts, u, opens):
            for t in range(ts.start, ts.stop):
                nc.tensor.matmul(
                    dst[:, t - ts.start, u * P : (u + 1) * P], src[:, t, :], ident[:], is_transpose=True,
                    start=opens and u == 0 and t == ts.start, stop=not opens and u == 1 and t == ts.stop - 1,
                )

        def carry(dst, h, ts, cols):
            nc.vector.scalar_tensor_tensor(
                dst, gate[h][:, ts, cols], 1.0, res_sb[h][:, ts, cols], ALU.subtract, ALU.mult
            )

        def candidates_rest(ts, n):
            ve = bank(n, [P, 2, PIECE])
            for t in range(ts.start, ts.stop):
                cols = slice(t * P, (t + 1) * P)
                weights = (
                    (wvd_codes[:, cols].bitcast(FP8X4), wvd_scale[:, cols]),
                    (w4_codes[:, 2 * t * P : 2 * (t + 1) * P].bitcast(FP4X4), w4_scale[:, cols]),
                )
                for c in range(0, PIECE, P):
                    run = slice(PIECE + c, PIECE + c + P)
                    for u, (codes, scale) in enumerate(weights):
                        nc.tensor.matmul_mx(
                            ve[:, t - ts.start, c : c + P], lhsT=codes, lhsT_scale=scale,
                            rhs=x_codes[1][:, run].bitcast(FP8X4), rhs_scale=x_scale[1][:, run],
                            start=u == 0, stop=u == 1,
                        )
            nc.scalar.activation(cand_rest[:, ts, :], ve[:], ACT.Tanh)

        def update(ts):
            nc.vector.scalar_tensor_tensor(
                y[1][:, ts, back], gate[1][:, ts, back], 1.0, cand_rest[:, ts, :], ALU.subtract, ALU.mult
            )

        def mix(h, ts, cols, first, second):
            nc.vector.tensor_tensor(y[h][:, ts, cols], first, second, ALU.subtract)

        def store(h, ts, cols):
            nc.sync.dma_start(y_rows[:, ts, h * HALF + cols.start : h * HALF + cols.stop], y[h][:, ts, cols])

        def woven(h, cols):
            c = max(c for c in y_bf if c <= h * HALF + cols.start)
            return y_bf[c][:, h * HALF + cols.start - c : h * HALF + cols.stop - c, :]

        def weave_y(copy, h, cols):
            weave(copy, woven(h, cols), y[h][:, :, cols])

        def quant_y(h, cols):
            whole = slice(h * HALF + cols.start, h * HALF + cols.stop)
            nc.vector.quantize_mx(
                y_codes[:, whole].bitcast(FP8X4), y_scale[:, whole], woven(h, cols).rearrange("p c t -> p (c t)")
            )

        def store_words(cols):
            nc.sync.dma_start(words[:, cols], y_codes[:, cols].bitcast(I32))

        def difference(n):
            nc.vector.tensor_tensor(step[:, n], res_t[n][:], cand[SUMMED[n]][:], ALU.subtract)

        def scaled(n, runs):
            ts = pairs[n]
            for us in runs:
                nc.vector.tensor_tensor(step[:, us, ts, :], gate_t[n][:, us], step[:, us, ts, :], ALU.mult)
                for u in range(us.start, us.stop):
                    turn_back(sums[n], step[:, u], ts, u, False)

        def leave(n):
            nc.scalar.copy(y[1][:, pairs[n], front], sums[n][:])
            store(1, pairs[n], front)

        def open_sum(n):
            dst = bank(SUMMED[n], [P, 2, PIECE])
            for u in range(2):
                turn_back(dst, cand[SUMMED[u]], pairs[n], u, True)
            return dst

        whole = slice(0, HALF)
        front, back = slice(0, PIECE), slice(PIECE, HALF)
        gates(0)
        candidates_near()
        for ts in pairs:
            carry(res_sb[0][:, ts, :], 0, ts, whole)
        for t in range(PACK):
            nc.vector.tensor_tensor(y[0][:, t, :], cand_near[:, t, :], gate[0][:, t, :], ALU.mult)
        gates(1)
        for b in SUMMED:
            candidates(b, b)
        res_t = [turn(res_sb[1][:, :, places(b)[1]], 2 + b) for b in SUMMED]
        for n, ts in enumerate(pairs):
            candidates_rest(ts, n)
        gate_t = [turn_pair(gate[1][:, :, front], ts, 2 + n) for n, ts in enumerate(pairs)]
        sums = [open_sum(n) for n in range(2)]
        mix(0, pairs[0], whole, y[0][:, pairs[0], :], res_sb[0][:, pairs[0], :])
        store(0, pairs[0], whole)
        for ts, cols in ((slice(2, 3), whole), (slice(3, 4), front), (slice(3, 4), back)):
            mix(0, ts, cols, y[0][:, ts, cols], res_sb[0][:, ts, cols])
        store(0, pairs[1], whole)
        carried = res_sb[0][:, :, front]
        nc.gpsimd.tensor_tensor(carried, gate[1][:, :, back], res_sb[1][:, :, back], ALU.mult)
        weave_y(nc.scalar.copy, 0, front)
        weave_y(nc.scalar.copy, 0, slice(PIECE, HALF - P))
        difference(0)
        difference(1)
        scaled(0, [slice(0, 1), slice(1, 2)])
        scaled(1, [slice(0, 2)])
        leave(0)
        leave(1)
        for b in SUMMED:
            weave_y(nc.scalar.copy, 1, places(b)[1])
        late = [places(b)[1] for b in (7, 6)]
        for ts in pairs:
            update(ts)
        for ts in pairs:
            mix(1, ts, back, carried[:, ts, :], y[1][:, ts, back])
        for ts in pairs:
            store(1, ts, back)
        y_bf[HALF - P] = tile("y_bf_back", [P, P, PACK], BF16, "step")
        weave_y(nc.vector.tensor_copy, 0, slice(HALF - P, HALF))
        weave_y(nc.scalar.copy, 1, late[0])
        quant_y(0, front)
        quant_y(0, slice(PIECE, HALF - P))
        quant_y(0, slice(HALF - P, HALF))
        store_words(whole)
        weave_y(nc.vector.tensor_copy, 1, late[1])
        quant_y(1, front)
        quant_y(1, back)
        store_words(slice(HALF, J))
        for q in range(4):
            queue = nc.sync if q == 0 else nc.scalar
            queue.dma_start(
                out_2[0, 4 * q : 4 * q + 4, :].bitcast(I32), y_scale[32 * q : 32 * q + 4, :].bitcast(I32)
            )
